import numpy as np
import ml_dtypes


def mxq(x, axis, fmt="e4m3"):
    dtype, down = {"e4m3": (ml_dtypes.float8_e4m3fn, 7), "e5m2": (ml_dtypes.float8_e5m2, 14)}[fmt]
    v = np.moveaxis(np.asarray(x, np.float32).astype(ml_dtypes.bfloat16).astype(np.float64), axis, -1)
    blocks = v.reshape(v.shape[:-1] + (-1, 32))
    amax = np.abs(blocks).max(-1, keepdims=True)
    byte = np.maximum(np.where(amax > 0, np.frexp(amax)[1] - 1 + 127, 0) - down, 1)
    scale = np.exp2(byte - 127.0)
    codes = (blocks / scale).astype(np.float32).astype(dtype).astype(np.float64)
    return np.moveaxis((codes * scale).reshape(v.shape), -1, axis)


WIDE = False


def mx_kscale(k):
    if not WIDE:
        return np.ones(k)
    levels = np.array([10, -10, 5, -5, 0])
    if k % 512:
        return np.exp2(np.random.permutation(np.resize(levels, k // 32))).repeat(32)
    a = np.empty((k // 512, 16))
    for p in range(k // 512):
        a[p, :8] = np.random.permutation(np.resize(levels, 8))
        for g in range(8):
            far = levels[np.abs(levels - a[p, g]) >= 10]
            a[p, g + 8] = far[np.random.randint(len(far))]
    return np.exp2(a.ravel()).repeat(32)


def f64(x):
    return np.asarray(x).astype(np.float64)


def striped(idx):
    return np.tile(idx.reshape(-1, 16).T, (8, 1)).astype(np.uint16)


def unstriped(offs):
    return offs[:16].T.reshape(-1).astype(np.int64)


E2M1 = np.array([0.0, 0.5, 1.0, 1.5, 2.0, 3.0, 4.0, 6.0, -0.0, -0.5, -1.0, -1.5, -2.0, -3.0, -4.0, -6.0])


def pack_weight(w, fmt):
    k, n = w.shape
    w = f64(np.asarray(w, np.float32).astype(ml_dtypes.bfloat16)).reshape(k // 32, 32, n)
    amax = np.abs(w).max(1)
    if fmt == "e4m3":
        byte = np.frexp(amax)[1] - 1 + 127 - 7
    else:
        mant, ex = np.frexp(amax / 6.0)
        byte = np.where(mant > 0.5, ex, ex - 1) + 127
    byte = np.clip(np.where(amax > 0, byte, 1), 1, 254)
    scaled = (w * np.exp2(127.0 - byte)[:, None, :]).reshape(k, n).astype(np.float32)
    by_word = np.ascontiguousarray(scaled.reshape(k // 512, 128, 4, n).transpose(0, 1, 3, 2))
    if fmt == "e4m3":
        words = by_word.astype(ml_dtypes.float8_e4m3fn).view(np.uint8)
    else:
        c = by_word.astype(ml_dtypes.float4_e2m1fn).view(np.uint8) & 0xF
        words = (c[..., 0::2] | (c[..., 1::2] << 4)).reshape(k // 512, 128, 2 * n)
    return np.ascontiguousarray(words), np.ascontiguousarray(byte.astype(np.uint8).reshape(k // 512, 16, n))


def unpack_weight(words, scales, fmt):
    g, _, n = scales.shape
    words = np.ascontiguousarray(words).reshape(g, 128, n, -1)
    if fmt == "e4m3":
        vals = words.view(ml_dtypes.float8_e4m3fn).astype(np.float64)
    else:
        nib = np.empty((g, 128, n, 4), np.uint8)
        nib[..., 0::2] = words & 0xF
        nib[..., 1::2] = words >> 4
        vals = E2M1[nib]
    vals = vals * np.repeat(np.exp2(scales.astype(np.float64) - 127.0), 8, axis=1)[..., None]
    return vals.transpose(0, 1, 3, 2).reshape(g * 512, n)


def relu2(v):
    return np.maximum(v, 0.0) ** 2


K, T, E, C, H, TOP, COPIES = 1024, 512, 4, 128, 512, 2, 384
PAD = 64


def by_expert(wq, xq):
    return np.concatenate([wq[e].T @ xq[:, e * C:(e + 1) * C] for e in range(E)], axis=1)


def setup_inputs():
    n = np.random.standard_normal
    s = mx_kscale(K)
    u = mx_kscale(H)
    left = TOP * T - E * C - COPIES
    deal = np.repeat(np.arange(E + 2), [C] * E + [COPIES, left]).reshape(TOP, T)[:, np.random.permutation(T)]
    deal = np.take_along_axis(deal, np.argsort(np.random.rand(TOP, T), axis=0), axis=0)
    for _ in range(8):
        s_, t_ = np.random.permutation(T).reshape(2, -1); r = np.random.randint(TOP, size=T // 2); x, y = deal[r, s_].copy(), deal[r, t_].copy()
        ok = ~((deal[:, s_] == y).any(0) | (deal[:, t_] == x).any(0)); deal[r[ok], s_[ok]] = y[ok]; deal[r[ok], t_[ok]] = x[ok]
    order = np.lexsort((np.random.rand(TOP * T), deal.reshape(-1)))[:E * C]
    slot_token = order % T
    pos = np.where(deal == E, E * C + np.arange(T), E * C + T + np.arange(T) % PAD).reshape(-1); pos[order] = np.arange(E * C); pos = pos.reshape(TOP, T)
    g = np.random.uniform(0.5, 1.5, (TOP, T)); g = g / g.sum(0)
    xf = n((K, T))
    x = pack_weight(xf * s[:, None], "e4m3")
    w1 = [pack_weight(m, "e4m3") for m in n((E, K, H)) / np.sqrt(K) / s[None, :, None] * u]
    w2 = [pack_weight(m, "e4m3") for m in n((E, H, K)) / np.sqrt(H) / u[None, :, None] ** 2]
    return {
        "x_words": x[0],
        "x_scales": x[1],
        "xr": (xf).astype(np.float32),
        "w1_words": np.stack([m[0] for m in w1]),
        "w1_scales": np.stack([m[1] for m in w1]),
        "w2_words": np.stack([m[0] for m in w2]),
        "w2_scales": np.stack([m[1] for m in w2]),
        "gate": np.stack([np.tile(r, (128, 1)) for r in g]).astype(np.float32),
        "offs": striped(slot_token),
        "pos1": striped(pos[0]),
        "pos2": striped(pos[1]),
    }


def reference(x_words, x_scales, xr, w1_words, w1_scales, w2_words, w2_scales, gate, offs, pos1, pos2):
    w1 = np.stack([unpack_weight(w1_words[e], w1_scales[e], "e4m3") for e in range(E)])
    w2 = np.stack([unpack_weight(w2_words[e], w2_scales[e], "e4m3") for e in range(E)])
    idx = unstriped(offs)
    xq = unpack_weight(x_words, x_scales, "e4m3")[:, idx]
    h = relu2(by_expert(w1, xq))
    y = by_expert(w2, mxq(h, 0, "e4m3"))
    y = np.concatenate([y, f64(xr), np.zeros((K, PAD))], axis=1)
    out = sum(f64(gate[r, :1]) * y[:, unstriped(p)] for r, p in enumerate((pos1, pos2)))
    return out

@@ -1,0 +1,256 @@
+from contextlib import ExitStack
+
+import concourse.mybir as mybir
+from concourse.masks import make_identity
+
+K, T, E, C, H, PAD = 1024, 512, 4, 128, 512, 64
+FLOPS = 2 * 2 * K * H * E * C
+
+F32 = mybir.dt.float32
+BF16 = mybir.dt.bfloat16
+I32 = mybir.dt.int32
+U32 = mybir.dt.uint32
+U16 = mybir.dt.uint16
+U8 = mybir.dt.uint8
+FP8X4 = mybir.dt.float8_e4m3fn_x4
+ACT = mybir.ActivationFunctionType
+ALU = mybir.AluOpType
+
+P = 128
+S = E * C
+WIN = S + T + PAD
+NB = K // P
+GATHER_CUTS = [(0, 128), (128, 256), (256, 512)]
+W2_CUTS = [(0, 1), (1, 2), (2, 4), (4, 8)]
+PE_ADD_BLOCKS = 7
+HALF = T // 2
+
+
+def tile_moe_cpy_mlp_relu2_kernel(
+    tc, x_words, x_scales, xr, w1_words, w1_scales, w2_words, w2_scales, gate, offs, pos1, pos2, out
+):
+    nc = tc.nc
+    with ExitStack() as ctx:
+        keep = ctx.enter_context(tc.tile_pool(name="keep", bufs=1))
+        ring = ctx.enter_context(tc.tile_pool(name="ring", bufs=3))
+        psum = ctx.enter_context(tc.psum_pool(name="psum", bufs=2))
+        psum_y = ctx.enter_context(tc.psum_pool(name="psum_y", bufs=4))
+
+        offs_sb = keep.tile([P, S // 16], U16, name="offs_sb")
+        pos_sb = [keep.tile([P, T // 16], U16, name=f"pos_sb{r}") for r in range(2)]
+        xw = keep.tile([P, 2 * T], U32, name="xw", align_bytes=64)
+        xs = keep.tile([P, T], U8, name="xs", align_bytes=64)
+        w1w = [keep.tile([P, 2, H], U32, name=f"w1w{e}", align_bytes=64) for e in range(E)]
+        w1s = [keep.tile([P, H], U8, name=f"w1s{h}", align_bytes=64) for h in range(2)]
+        w2w = [keep.tile([P, E, (b1 - b0) * P], U32, name=f"w2w{b0}", align_bytes=64) for b0, b1 in W2_CUTS]
+        w2s = keep.tile([P, K], U8, name="w2s", align_bytes=64)
+        gate_sb = [keep.tile([P, T], F32, name=f"gate_sb{r}") for r in range(2)]
+        ywin = [keep.tile([P, WIN], F32, name=f"ywin{b}") for b in range(NB)]
+        zeros = keep.tile([P, PAD], F32, name="zeros")
+        ident = keep.tile([P, P], F32, name="ident")
+
+        for plane in (xs, w1s[0], w1s[1], w2s):
+            nc.vector.memset(plane[:].bitcast(I32), 0)
+        nc.vector.memset(zeros[:], 0.0)
+        make_identity(nc, ident[:])
+
+        def load_w1(e):
+            nc.sync.dma_start(
+                out=w1w[e][:].bitcast(I32),
+                in_=w1_words[e].rearrange("s p i d -> p s (i d)").bitcast(I32),
+            )
+
+        def load_w2(c):
+            b0, b1 = W2_CUTS[c]
+            src = w2_words.rearrange("e s p n d -> p (e s) (n d)").bitcast(I32)
+            nc.sync.dma_start(out=w2w[c][:].bitcast(I32), in_=src[:, :, b0 * P : b1 * P])
+
+        def load_xr(b):
+            nc.sync.dma_start(out=ywin[b][:, S : S + T], in_=xr[b * P : (b + 1) * P, :])
+
+        def load_planes(queue, plane, rows):
+            count = rows.shape[0]
+            for q in range(4):
+                queue.dma_start(
+                    out=plane[32 * q : 32 * q + 4 * count, :].bitcast(I32),
+                    in_=rows[:, 4 * q : 4 * q + 4, :].bitcast(I32),
+                )
+
+        w1_rows = w1_scales.rearrange("e s b i -> (e s) b i")
+        nc.sync.dma_start(out=offs_sb[:], in_=offs)
+        load_planes(nc.scalar, xs, x_scales)
+        nc.sync.dma_start(
+            out=xw[:].bitcast(I32).rearrange("p (s t) -> p s t", s=2),
+            in_=x_words.rearrange("s p t d -> p s (t d)").bitcast(I32),
+        )
+        load_w1(0)
+        load_w1(1)
+        load_planes(nc.scalar, w1s[0], w1_rows[0:4])
+        load_planes(nc.gpsimd, w1s[1], w1_rows[4:8])
+        load_w1(2)
+        load_w1(3)
+        load_planes(nc.gpsimd, w2s, w2_scales.rearrange("e s b n -> (e s) b n"))
+        load_w2(0)
+        nc.sync.dma_start(out=pos_sb[0][:], in_=pos1)
+        load_xr(0)
+        nc.sync.dma_start(out=gate_sb[0][:], in_=gate[0])
+        nc.sync.dma_start(out=pos_sb[1][:], in_=pos2)
+        nc.sync.dma_start(out=gate_sb[1][:], in_=gate[1])
+        for c, (b0, b1) in enumerate(W2_CUTS):
+            if c > 0:
+                load_w2(c)
+                for b in range(b0, b1):
+                    load_xr(b)
+
+        for b in range(NB):
+            nc.scalar.copy(ywin[b][:, S + T : WIN], zeros[:])
+
+        slot_words = {}
+        slot_scales = {}
+
+        def gather_tokens(lo, hi):
+            picks = offs_sb[:, lo // 16 : hi // 16]
+            words = []
+            for s in range(2):
+                g = keep.tile([P, hi - lo], U32, name=f"xg{lo}_{s}", align_bytes=64)
+                nc.vector.tensor_copy(g[:], xw[:, s * T : (s + 1) * T].indirect(picks))
+                words.append(g)
+            gs = keep.tile([P, hi - lo], U8, name=f"xgs{lo}", align_bytes=64)
+            nc.vector.tensor_copy(gs[:], xs[:].indirect(picks))
+            for e in range(lo // C, hi // C):
+                cols = slice(e * C - lo, (e + 1) * C - lo)
+                slot_words[e] = [words[s][:, cols] for s in range(2)]
+                slot_scales[e] = [gs[4 * s : P, cols] for s in range(2)]
+
+        h_words = [keep.tile([P, C], U32, name=f"h_words{e}", align_bytes=64) for e in range(E)]
+        h_scales = [keep.tile([P, C], U8, name=f"h_scales{e}", align_bytes=64) for e in range(E)]
+        h_bf = {}
+        relu_out = {}
+
+        def first_layer(e):
+            acc = psum.tile([P, H], F32, name="acc", tag="first")
+            for s in range(2):
+                j = 2 * (e % 2) + s
+                nc.tensor.matmul_mx(
+                    out=acc[:],
+                    lhsT=slot_words[e][s].bitcast(FP8X4),
+                    lhsT_scale=slot_scales[e][s],
+                    rhs=w1w[e][:, s, :].bitcast(FP8X4),
+                    rhs_scale=w1s[e // 2][4 * j : P, :],
+                    start=(s == 0),
+                    stop=(s == 1),
+                )
+            pos_part = ring.tile([P, 4, P], F32, name="pos_part")
+            src = acc[:].rearrange("p (m d) -> p d m", d=4)
+            if e < 2:
+                nc.scalar.activation(pos_part[:], src, ACT.Relu)
+            else:
+                nc.vector.tensor_scalar_max(pos_part[:], src, 0.0)
+            relu_out[e] = pos_part
+
+        def square(e):
+            turned = psum.tile([P, 4, C], F32, name="turned", tag="second")
+            for d in range(4):
+                nc.tensor.transpose(turned[:, d, :], relu_out[e][:, d, :], ident[:])
+            hb = ring.tile([P, C, 4], BF16, name="hb", align_bytes=64)
+            nc.scalar.activation(hb[:], turned[:].rearrange("p d u -> p u d"), ACT.Square)
+            h_bf[e] = hb
+
+        def quantise(e):
+            nc.vector.quantize_mx(
+                out=h_words[e][:].bitcast(FP8X4),
+                scales=h_scales[e][:],
+                in_=h_bf[e][:].rearrange("p u d -> p (u d)"),
+            )
+
+        def second_layer(b, experts, engine):
+            c = [i for i, (b0, b1) in enumerate(W2_CUTS) if b0 <= b < b1][0]
+            local = slice((b - W2_CUTS[c][0]) * P, (b - W2_CUTS[c][0] + 1) * P)
+            ysum = psum_y.tile([P, len(experts) * C], F32, name="ysum")
+            for i, e in enumerate(experts):
+                nc.tensor.matmul_mx(
+                    out=ysum[:, i * C : (i + 1) * C],
+                    lhsT=w2w[c][:, e, local].bitcast(FP8X4),
+                    lhsT_scale=w2s[4 * e : P, b * P : (b + 1) * P],
+                    rhs=h_words[e][:].bitcast(FP8X4),
+                    rhs_scale=h_scales[e][:],
+                    start=True,
+                    stop=True,
+                )
+            dst = ywin[b][:, experts[0] * C : (experts[-1] + 1) * C]
+            if engine == "vector":
+                nc.vector.tensor_copy(dst, ysum[:])
+            else:
+                nc.scalar.copy(dst, ysum[:])
+
+        def pick(b, r, lo, hi):
+            part = ring.tile([P, hi - lo], F32, name=f"part{r}", tag=f"part{r}")
+            nc.vector.tensor_tensor(
+                part[:], ywin[b][:].indirect(pos_sb[r][:, lo // 16 : hi // 16]), gate_sb[r][:, lo:hi], ALU.mult
+            )
+            return part
+
+        def add_on_tensor(b, parts):
+            res = ring.tile([P, T], F32, name="res")
+            for h in range(2):
+                by_token = psum.tile([P, 2, P], F32, name="by_token", tag="first")
+                for c in range(2):
+                    cols = slice(h * HALF + c * P, h * HALF + (c + 1) * P)
+                    for r in range(2):
+                        nc.tensor.matmul(
+                            by_token[:, c, :], parts[r][:, cols], ident[:],
+                            start=(r == 0), stop=(r == 1), is_transpose=True,
+                        )
+                summed = ring.tile([P, 2, P], F32, name="summed")
+                nc.scalar.copy(summed[:], by_token[:])
+                by_row = psum.tile([P, 2, P], F32, name="by_row", tag="second")
+                for c in range(2):
+                    nc.tensor.transpose(by_row[:, c, :], summed[:, c, :], ident[:])
+                nc.scalar.copy(res[:, h * HALF : (h + 1) * HALF], by_row[:].rearrange("p c t -> p (c t)"))
+            nc.sync.dma_start(out=out[b * P : (b + 1) * P, :], in_=res[:])
+
+        def add_on_vector(b, parts, lo, hi):
+            res = ring.tile([P, hi - lo], F32, name="res_v")
+            nc.vector.tensor_tensor(res[:], parts[0][:], parts[1][:], ALU.add)
+            nc.sync.dma_start(out=out[b * P : (b + 1) * P, lo:hi], in_=res[:])
+
+        gather_tokens(*GATHER_CUTS[0])
+        first_layer(0)
+        gather_tokens(*GATHER_CUTS[1])
+        first_layer(1)
+        square(0)
+        gather_tokens(*GATHER_CUTS[2])
+        quantise(0)
+        square(1)
+        first_layer(2)
+        quantise(1)
+        first_layer(3)
+        square(2)
+        quantise(2)
+        square(3)
+        second_layer(0, [0, 1, 2], "scalar")
+        quantise(3)
+        second_layer(0, [3], "vector")
+        second_layer(1, [0, 1, 2, 3], "scalar")
+        waiting = None
+        for b in range(NB - 1):
+            first = pick(b, 0, 0, T)
+            if waiting is not None:
+                add_on_vector(b - 1, waiting, 0, T)
+                waiting = None
+            parts = [first, pick(b, 1, 0, T)]
+            if b + 2 < NB:
+                second_layer(b + 2, [0, 1, 2, 3], "scalar")
+            if b < PE_ADD_BLOCKS:
+                add_on_tensor(b, parts)
+            else:
+                waiting = parts
+        last = NB - 1
+        a0 = pick(last, 0, 0, HALF)
+        if waiting is not None:
+            add_on_vector(last - 1, waiting, 0, T)
+        b0 = pick(last, 1, 0, HALF)
+        a1 = pick(last, 0, HALF, T)
+        add_on_vector(last, [a0, b0], 0, HALF)
+        b1 = pick(last, 1, HALF, T)
+        add_on_vector(last, [a1, b1], HALF, T)

@@ -1,7 +1,6 @@
 from contextlib import ExitStack
 
 import concourse.mybir as mybir
-from concourse.masks import make_identity
 
 K, T, E, C, H, PAD = 1024, 512, 4, 128, 512, 64
 FLOPS = 2 * 2 * K * H * E * C
@@ -21,6 +20,8 @@ S = E * C
 WIN = S + T + PAD
 NB = K // P
 GATHER_CUTS = [(0, 128), (128, 256), (256, 512)]
+W1_CUTS = [(0, 1), (1, 2), (2, 3), (3, 4)]
+WARM = 7
 W2_CUTS = [(0, 1), (1, 2), (2, 4), (4, 8)]
 PE_ADD_BLOCKS = 7
 HALF = T // 2
@@ -40,25 +41,33 @@ def tile_moe_cpy_mlp_relu2_kernel(
         pos_sb = [keep.tile([P, T // 16], U16, name=f"pos_sb{r}") for r in range(2)]
         xw = keep.tile([P, 2 * T], U32, name="xw", align_bytes=64)
         xs = keep.tile([P, T], U8, name="xs", align_bytes=64)
-        w1w = [keep.tile([P, 2, H], U32, name=f"w1w{e}", align_bytes=64) for e in range(E)]
+        w1w = [keep.tile([P, 2 * (e1 - e0), H], U32, name=f"w1w{e0}", align_bytes=64) for e0, e1 in W1_CUTS]
         w1s = [keep.tile([P, H], U8, name=f"w1s{h}", align_bytes=64) for h in range(2)]
         w2w = [keep.tile([P, E, (b1 - b0) * P], U32, name=f"w2w{b0}", align_bytes=64) for b0, b1 in W2_CUTS]
         w2s = keep.tile([P, K], U8, name="w2s", align_bytes=64)
-        gate_sb = [keep.tile([P, T], F32, name=f"gate_sb{r}") for r in range(2)]
+        gate_sb = keep.tile([P, 2, T], F32, name="gate_sb")
         ywin = [keep.tile([P, WIN], F32, name=f"ywin{b}") for b in range(NB)]
         zeros = keep.tile([P, PAD], F32, name="zeros")
         ident = keep.tile([P, P], F32, name="ident")
 
-        for plane in (xs, w1s[0], w1s[1], w2s):
+        for plane in (xs, w1s[1], w2s):
             nc.vector.memset(plane[:].bitcast(I32), 0)
         nc.vector.memset(zeros[:], 0.0)
-        make_identity(nc, ident[:])
+        ones = keep.tile([P, 32], F32, name="ones")
+        column = keep.tile([P, 32], F32, name="column", align_bytes=64)
+        row = keep.tile([P, 32], F32, name="row", align_bytes=64)
+        nc.vector.memset(ones[:], 1.0)
+        nc.vector.memset(ident[:], 0.0)
+        nc.vector.tensor_tensor_scan(column[:], ones[:], ones[:], 0.0, ALU.mult, ALU.add)
+        nc.vector.transpose(row[:], column[:])
+        for q in range(4):
+            quad = slice(32 * q, 32 * q + 32)
+            nc.vector.tensor_tensor(ident[quad, quad], column[quad, :], row[quad, :], ALU.is_equal)
 
-        def load_w1(e):
-            nc.sync.dma_start(
-                out=w1w[e][:].bitcast(I32),
-                in_=w1_words[e].rearrange("s p i d -> p s (i d)").bitcast(I32),
-            )
+        def load_w1(c):
+            e0, e1 = W1_CUTS[c]
+            src = w1_words.rearrange("e s p i d -> p (e s) (i d)").bitcast(I32)
+            nc.sync.dma_start(out=w1w[c][:].bitcast(I32), in_=src[:, 2 * e0 : 2 * e1, :])
 
         def load_w2(c):
             b0, b1 = W2_CUTS[c]
@@ -77,25 +86,24 @@ def tile_moe_cpy_mlp_relu2_kernel(
                 )
 
         w1_rows = w1_scales.rearrange("e s b i -> (e s) b i")
-        nc.sync.dma_start(out=offs_sb[:], in_=offs)
-        load_planes(nc.scalar, xs, x_scales)
         nc.sync.dma_start(
             out=xw[:].bitcast(I32).rearrange("p (s t) -> p s t", s=2),
             in_=x_words.rearrange("s p t d -> p s (t d)").bitcast(I32),
         )
+        nc.sync.dma_start(out=offs_sb[:], in_=offs)
+        load_planes(nc.sync, w1s[0], w1_rows)
         load_w1(0)
         load_w1(1)
-        load_planes(nc.scalar, w1s[0], w1_rows[0:4])
-        load_planes(nc.gpsimd, w1s[1], w1_rows[4:8])
+        load_planes(nc.sync, xs, x_scales)
         load_w1(2)
         load_w1(3)
-        load_planes(nc.gpsimd, w2s, w2_scales.rearrange("e s b n -> (e s) b n"))
+        load_planes(nc.sync, w1s[1], w1_rows[4:8])
+        load_planes(nc.sync, w2s, w2_scales.rearrange("e s b n -> (e s) b n"))
         load_w2(0)
-        nc.sync.dma_start(out=pos_sb[0][:], in_=pos1)
         load_xr(0)
-        nc.sync.dma_start(out=gate_sb[0][:], in_=gate[0])
+        nc.sync.dma_start(out=gate_sb[:], in_=gate.rearrange("r p t -> p r t"))
+        nc.sync.dma_start(out=pos_sb[0][:], in_=pos1)
         nc.sync.dma_start(out=pos_sb[1][:], in_=pos2)
-        nc.sync.dma_start(out=gate_sb[1][:], in_=gate[1])
         for c, (b0, b1) in enumerate(W2_CUTS):
             if c > 0:
                 load_w2(c)
@@ -108,26 +116,29 @@ def tile_moe_cpy_mlp_relu2_kernel(
         slot_words = {}
         slot_scales = {}
 
-        def gather_tokens(lo, hi):
+        def gather_words(lo, hi):
             picks = offs_sb[:, lo // 16 : hi // 16]
             words = []
             for s in range(2):
                 g = keep.tile([P, hi - lo], U32, name=f"xg{lo}_{s}", align_bytes=64)
                 nc.vector.tensor_copy(g[:], xw[:, s * T : (s + 1) * T].indirect(picks))
                 words.append(g)
-            gs = keep.tile([P, hi - lo], U8, name=f"xgs{lo}", align_bytes=64)
-            nc.vector.tensor_copy(gs[:], xs[:].indirect(picks))
             for e in range(lo // C, hi // C):
-                cols = slice(e * C - lo, (e + 1) * C - lo)
-                slot_words[e] = [words[s][:, cols] for s in range(2)]
-                slot_scales[e] = [gs[4 * s : P, cols] for s in range(2)]
+                slot_words[e] = [words[s][:, e * C - lo : (e + 1) * C - lo] for s in range(2)]
+
+        def gather_scales(lo, hi):
+            gs = keep.tile([P, hi - lo], U8, name=f"xgs{lo}", align_bytes=64)
+            nc.vector.tensor_copy(gs[:], xs[:].indirect(offs_sb[:, lo // 16 : hi // 16]))
+            for e in range(lo // C, hi // C):
+                slot_scales[e] = [gs[4 * s : P, e * C - lo : (e + 1) * C - lo] for s in range(2)]
 
         h_words = [keep.tile([P, C], U32, name=f"h_words{e}", align_bytes=64) for e in range(E)]
-        h_scales = [keep.tile([P, C], U8, name=f"h_scales{e}", align_bytes=64) for e in range(E)]
+        h_scales = keep.tile([P, C], U8, name="h_scales", align_bytes=64)
         h_bf = {}
         relu_out = {}
 
         def first_layer(e):
+            c = [i for i, (e0, e1) in enumerate(W1_CUTS) if e0 <= e < e1][0]
             acc = psum.tile([P, H], F32, name="acc", tag="first")
             for s in range(2):
                 j = 2 * (e % 2) + s
@@ -135,31 +146,31 @@ def tile_moe_cpy_mlp_relu2_kernel(
                     out=acc[:],
                     lhsT=slot_words[e][s].bitcast(FP8X4),
                     lhsT_scale=slot_scales[e][s],
-                    rhs=w1w[e][:, s, :].bitcast(FP8X4),
+                    rhs=w1w[c][:, 2 * (e - W1_CUTS[c][0]) + s, :].bitcast(FP8X4),
                     rhs_scale=w1s[e // 2][4 * j : P, :],
                     start=(s == 0),
                     stop=(s == 1),
                 )
-            pos_part = ring.tile([P, 4, P], F32, name="pos_part")
+            pos_part = keep.tile([P, 4, P], F32, name=f"pos_part{e}")
             src = acc[:].rearrange("p (m d) -> p d m", d=4)
-            if e < 2:
+            if e < 1:
                 nc.scalar.activation(pos_part[:], src, ACT.Relu)
             else:
                 nc.vector.tensor_scalar_max(pos_part[:], src, 0.0)
             relu_out[e] = pos_part
 
         def square(e):
-            turned = psum.tile([P, 4, C], F32, name="turned", tag="second")
+            turned = psum_y.tile([P, 4, C], F32, name="turned", tag="ysum")
             for d in range(4):
                 nc.tensor.transpose(turned[:, d, :], relu_out[e][:, d, :], ident[:])
-            hb = ring.tile([P, C, 4], BF16, name="hb", align_bytes=64)
+            hb = keep.tile([P, C, 4], BF16, name=f"hb{e}", align_bytes=64)
             nc.scalar.activation(hb[:], turned[:].rearrange("p d u -> p u d"), ACT.Square)
             h_bf[e] = hb
 
         def quantise(e):
             nc.vector.quantize_mx(
                 out=h_words[e][:].bitcast(FP8X4),
-                scales=h_scales[e][:],
+                scales=h_scales[4 * e : P, :],
                 in_=h_bf[e][:].rearrange("p u d -> p (u d)"),
             )
 
@@ -173,7 +184,7 @@ def tile_moe_cpy_mlp_relu2_kernel(
                     lhsT=w2w[c][:, e, local].bitcast(FP8X4),
                     lhsT_scale=w2s[4 * e : P, b * P : (b + 1) * P],
                     rhs=h_words[e][:].bitcast(FP8X4),
-                    rhs_scale=h_scales[e][:],
+                    rhs_scale=h_scales[4 * e : P, :],
                     start=True,
                     stop=True,
                 )
@@ -186,7 +197,7 @@ def tile_moe_cpy_mlp_relu2_kernel(
         def pick(b, r, lo, hi):
             part = ring.tile([P, hi - lo], F32, name=f"part{r}", tag=f"part{r}")
             nc.vector.tensor_tensor(
-                part[:], ywin[b][:].indirect(pos_sb[r][:, lo // 16 : hi // 16]), gate_sb[r][:, lo:hi], ALU.mult
+                part[:], ywin[b][:].indirect(pos_sb[r][:, lo // 16 : hi // 16]), gate_sb[:, r, lo:hi], ALU.mult
             )
             return part
 
@@ -214,23 +225,34 @@ def tile_moe_cpy_mlp_relu2_kernel(
             nc.vector.tensor_tensor(res[:], parts[0][:], parts[1][:], ALU.add)
             nc.sync.dma_start(out=out[b * P : (b + 1) * P, lo:hi], in_=res[:])
 
-        gather_tokens(*GATHER_CUTS[0])
+        for i in range(WARM):
+            idle = psum_y.tile([P, 256], F32, name="ysum")
+            nc.tensor.matmul_mx(
+                out=idle[:],
+                lhsT=w1w[0][:, 0, 0:P].bitcast(FP8X4),
+                lhsT_scale=w1s[0][:, 0:P],
+                rhs=w1w[0][:, 0, 0:256].bitcast(FP8X4),
+                rhs_scale=w1s[0][:, 0:256],
+                start=True,
+                stop=True,
+            )
+        gather_words(0, S // 2)
+        gather_words(S // 2, S)
+        gather_scales(*GATHER_CUTS[0])
         first_layer(0)
-        gather_tokens(*GATHER_CUTS[1])
+        gather_scales(*GATHER_CUTS[1])
         first_layer(1)
+        gather_scales(*GATHER_CUTS[2])
         square(0)
-        gather_tokens(*GATHER_CUTS[2])
-        quantise(0)
-        square(1)
         first_layer(2)
-        quantise(1)
         first_layer(3)
+        square(1)
         square(2)
-        quantise(2)
         square(3)
-        second_layer(0, [0, 1, 2], "scalar")
-        quantise(3)
-        second_layer(0, [3], "vector")
+        for e in range(E):
+            quantise(e)
+        second_layer(0, [0, 1], "scalar")
+        second_layer(0, [2, 3], "vector")
         second_layer(1, [0, 1, 2, 3], "scalar")
         waiting = None
         for b in range(NB - 1):

@@ -19,12 +19,11 @@ P = 128
 S = E * C
 WIN = S + T + PAD
 NB = K // P
-GATHER_CUTS = [(0, 128), (128, 256), (256, 512)]
-W1_CUTS = [(0, 1), (1, 2), (2, 3), (3, 4)]
-WARM = 7
-W2_CUTS = [(0, 1), (1, 2), (2, 4), (4, 8)]
-PE_ADD_BLOCKS = 7
-HALF = T // 2
+W2_CUTS = [(0, 2), (2, 5), (5, 8)]
+HALF_H = H // 2
+HALF_T = T // 2
+TAIL = 128
+WARM = 4
 
 
 def tile_moe_cpy_mlp_relu2_kernel(
@@ -33,26 +32,34 @@ def tile_moe_cpy_mlp_relu2_kernel(
     nc = tc.nc
     with ExitStack() as ctx:
         keep = ctx.enter_context(tc.tile_pool(name="keep", bufs=1))
-        ring = ctx.enter_context(tc.tile_pool(name="ring", bufs=3))
-        psum = ctx.enter_context(tc.psum_pool(name="psum", bufs=2))
-        psum_y = ctx.enter_context(tc.psum_pool(name="psum_y", bufs=4))
+        psum = ctx.enter_context(tc.psum_pool(name="psum", bufs=1))
+
+        def bank(n, shape):
+            return psum.tile(shape, F32, name=f"bank{n}", tag=f"bank{n}")
 
         offs_sb = keep.tile([P, S // 16], U16, name="offs_sb")
         pos_sb = [keep.tile([P, T // 16], U16, name=f"pos_sb{r}") for r in range(2)]
         xw = keep.tile([P, 2 * T], U32, name="xw", align_bytes=64)
         xs = keep.tile([P, T], U8, name="xs", align_bytes=64)
-        w1w = [keep.tile([P, 2 * (e1 - e0), H], U32, name=f"w1w{e0}", align_bytes=64) for e0, e1 in W1_CUTS]
+        w1w = [keep.tile([P, 2, H], U32, name=f"w1w{e}", align_bytes=64) for e in range(E - 1)]
+        w1w_last = [keep.tile([P, 2, HALF_H], U32, name=f"w1w_last{h}", align_bytes=64) for h in range(2)]
         w1s = [keep.tile([P, H], U8, name=f"w1s{h}", align_bytes=64) for h in range(2)]
         w2w = [keep.tile([P, E, (b1 - b0) * P], U32, name=f"w2w{b0}", align_bytes=64) for b0, b1 in W2_CUTS]
         w2s = keep.tile([P, K], U8, name="w2s", align_bytes=64)
-        gate_sb = keep.tile([P, 2, T], F32, name="gate_sb")
+        gate_sb = [keep.tile([P, T], F32, name=f"gate_sb{r}") for r in range(2)]
         ywin = [keep.tile([P, WIN], F32, name=f"ywin{b}") for b in range(NB)]
         zeros = keep.tile([P, PAD], F32, name="zeros")
         ident = keep.tile([P, P], F32, name="ident")
 
+        nc.gpsimd.memset(w1s[0][:].bitcast(I32), 0)
         for plane in (xs, w1s[1], w2s):
             nc.vector.memset(plane[:].bitcast(I32), 0)
         nc.vector.memset(zeros[:], 0.0)
+        warm_in = keep.tile([P, 4 * H], BF16, name="warm_in", align_bytes=64)
+        warm_words = keep.tile([P, H], U32, name="warm_words", align_bytes=64)
+        warm_scales = keep.tile([P, H], U8, name="warm_scales", align_bytes=64)
+        nc.gpsimd.memset(warm_in[:].bitcast(I32), 0)
+        nc.vector.quantize_mx(out=warm_words[:].bitcast(FP8X4), scales=warm_scales[:], in_=warm_in[:])
         ones = keep.tile([P, 32], F32, name="ones")
         column = keep.tile([P, 32], F32, name="column", align_bytes=64)
         row = keep.tile([P, 32], F32, name="row", align_bytes=64)
@@ -64,127 +71,121 @@ def tile_moe_cpy_mlp_relu2_kernel(
             quad = slice(32 * q, 32 * q + 32)
             nc.vector.tensor_tensor(ident[quad, quad], column[quad, :], row[quad, :], ALU.is_equal)
 
-        def load_w1(c):
-            e0, e1 = W1_CUTS[c]
-            src = w1_words.rearrange("e s p i d -> p (e s) (i d)").bitcast(I32)
-            nc.sync.dma_start(out=w1w[c][:].bitcast(I32), in_=src[:, 2 * e0 : 2 * e1, :])
+        w1_src = w1_words.rearrange("e s p i d -> e p s (i d)").bitcast(I32)
+        w2_src = w2_words.rearrange("e s p n d -> p (e s) (n d)").bitcast(I32)
 
         def load_w2(c):
             b0, b1 = W2_CUTS[c]
-            src = w2_words.rearrange("e s p n d -> p (e s) (n d)").bitcast(I32)
-            nc.sync.dma_start(out=w2w[c][:].bitcast(I32), in_=src[:, :, b0 * P : b1 * P])
+            nc.sync.dma_start(out=w2w[c][:].bitcast(I32), in_=w2_src[:, :, b0 * P : b1 * P])
 
         def load_xr(b):
             nc.sync.dma_start(out=ywin[b][:, S : S + T], in_=xr[b * P : (b + 1) * P, :])
 
-        def load_planes(queue, plane, rows):
+        def load_planes(queue, plane, rows, quadrants):
             count = rows.shape[0]
-            for q in range(4):
+            for q in quadrants:
                 queue.dma_start(
                     out=plane[32 * q : 32 * q + 4 * count, :].bitcast(I32),
                     in_=rows[:, 4 * q : 4 * q + 4, :].bitcast(I32),
                 )
 
+        def clear_zero_expert(b):
+            nc.scalar.activation(ywin[b][:, S + T : WIN], zeros[:], ACT.Square)
+
         w1_rows = w1_scales.rearrange("e s b i -> (e s) b i")
+        nc.sync.dma_start(out=offs_sb[:], in_=offs)
+        load_planes(nc.sync, w1s[0], w1_rows[0:4], range(2))
+        load_planes(nc.sync, xs, x_scales, range(4))
         nc.sync.dma_start(
             out=xw[:].bitcast(I32).rearrange("p (s t) -> p s t", s=2),
             in_=x_words.rearrange("s p t d -> p s (t d)").bitcast(I32),
         )
-        nc.sync.dma_start(out=offs_sb[:], in_=offs)
-        load_planes(nc.sync, w1s[0], w1_rows)
-        load_w1(0)
-        load_w1(1)
-        load_planes(nc.sync, xs, x_scales)
-        load_w1(2)
-        load_w1(3)
-        load_planes(nc.sync, w1s[1], w1_rows[4:8])
-        load_planes(nc.sync, w2s, w2_scales.rearrange("e s b n -> (e s) b n"))
+        load_planes(nc.sync, w1s[0], w1_rows[0:4], range(2, 4))
+        for e in range(E - 1):
+            if e == 2:
+                load_planes(nc.sync, w1s[1], w1_rows[4:8], range(4))
+            nc.sync.dma_start(out=w1w[e][:].bitcast(I32), in_=w1_src[e])
+        for h in range(2):
+            nc.sync.dma_start(
+                out=w1w_last[h][:].bitcast(I32), in_=w1_src[E - 1][:, :, h * HALF_H : (h + 1) * HALF_H]
+            )
+        load_planes(nc.sync, w2s, w2_scales.rearrange("e s b n -> (e s) b n"), range(4))
         load_w2(0)
         load_xr(0)
-        nc.sync.dma_start(out=gate_sb[:], in_=gate.rearrange("r p t -> p r t"))
-        nc.sync.dma_start(out=pos_sb[0][:], in_=pos1)
-        nc.sync.dma_start(out=pos_sb[1][:], in_=pos2)
-        for c, (b0, b1) in enumerate(W2_CUTS):
-            if c > 0:
-                load_w2(c)
-                for b in range(b0, b1):
-                    load_xr(b)
+        for r, pos in enumerate((pos1, pos2)):
+            nc.sync.dma_start(out=pos_sb[r][:], in_=pos)
+            nc.sync.dma_start(out=gate_sb[r][:], in_=gate[r])
+        load_xr(1)
+        load_w2(1)
+        load_xr(2)
+        load_w2(2)
+        for b in range(3, NB):
+            load_xr(b)
 
         for b in range(NB):
-            nc.scalar.copy(ywin[b][:, S + T : WIN], zeros[:])
+            clear_zero_expert(b)
 
         slot_words = {}
         slot_scales = {}
 
-        def gather_words(lo, hi):
-            picks = offs_sb[:, lo // 16 : hi // 16]
-            words = []
+        def gather_slots(e):
+            picks = offs_sb[:, e * C // 16 : (e + 1) * C // 16]
+            slot_words[e] = []
             for s in range(2):
-                g = keep.tile([P, hi - lo], U32, name=f"xg{lo}_{s}", align_bytes=64)
+                g = keep.tile([P, C], U32, name=f"xg{e}_{s}", align_bytes=64)
                 nc.vector.tensor_copy(g[:], xw[:, s * T : (s + 1) * T].indirect(picks))
-                words.append(g)
-            for e in range(lo // C, hi // C):
-                slot_words[e] = [words[s][:, e * C - lo : (e + 1) * C - lo] for s in range(2)]
-
-        def gather_scales(lo, hi):
-            gs = keep.tile([P, hi - lo], U8, name=f"xgs{lo}", align_bytes=64)
-            nc.vector.tensor_copy(gs[:], xs[:].indirect(offs_sb[:, lo // 16 : hi // 16]))
-            for e in range(lo // C, hi // C):
-                slot_scales[e] = [gs[4 * s : P, e * C - lo : (e + 1) * C - lo] for s in range(2)]
+                slot_words[e].append(g)
+            gs = keep.tile([P, C], U8, name=f"xgs{e}", align_bytes=64)
+            nc.vector.tensor_copy(gs[:], xs[:].indirect(picks))
+            slot_scales[e] = gs
 
         h_words = [keep.tile([P, C], U32, name=f"h_words{e}", align_bytes=64) for e in range(E)]
-        h_scales = keep.tile([P, C], U8, name="h_scales", align_bytes=64)
-        h_bf = {}
-        relu_out = {}
+        h_scales = [keep.tile([P, C], U8, name=f"h_scales{e}", align_bytes=64) for e in range(E)]
+        relu_out = [keep.tile([P, 4, P], F32, name=f"relu_out{e}") for e in range(E)]
+        h_bf = [keep.tile([P, C, 4], BF16, name=f"h_bf{e}", align_bytes=64) for e in range(E)]
 
-        def first_layer(e):
-            c = [i for i, (e0, e1) in enumerate(W1_CUTS) if e0 <= e < e1][0]
-            acc = psum.tile([P, H], F32, name="acc", tag="first")
+        def first_layer(e, words, lo, hi, n):
+            acc = bank(n, [P, hi - lo])
             for s in range(2):
                 j = 2 * (e % 2) + s
                 nc.tensor.matmul_mx(
                     out=acc[:],
-                    lhsT=slot_words[e][s].bitcast(FP8X4),
-                    lhsT_scale=slot_scales[e][s],
-                    rhs=w1w[c][:, 2 * (e - W1_CUTS[c][0]) + s, :].bitcast(FP8X4),
-                    rhs_scale=w1s[e // 2][4 * j : P, :],
+                    lhsT=slot_words[e][s][:].bitcast(FP8X4),
+                    lhsT_scale=slot_scales[e][4 * s : P, :],
+                    rhs=words[:, s, :].bitcast(FP8X4),
+                    rhs_scale=w1s[e // 2][4 * j : P, lo:hi],
                     start=(s == 0),
                     stop=(s == 1),
                 )
-            pos_part = keep.tile([P, 4, P], F32, name=f"pos_part{e}")
             src = acc[:].rearrange("p (m d) -> p d m", d=4)
-            if e < 1:
-                nc.scalar.activation(pos_part[:], src, ACT.Relu)
+            dst = relu_out[e][:, :, lo // 4 : hi // 4]
+            if e < 2:
+                nc.scalar.activation(dst, src, ACT.Relu)
             else:
-                nc.vector.tensor_scalar_max(pos_part[:], src, 0.0)
-            relu_out[e] = pos_part
+                nc.vector.tensor_scalar_max(dst, src, 0.0)
 
-        def square(e):
-            turned = psum_y.tile([P, 4, C], F32, name="turned", tag="ysum")
+        def square(e, n):
+            turned = bank(n, [P, 4, C])
             for d in range(4):
                 nc.tensor.transpose(turned[:, d, :], relu_out[e][:, d, :], ident[:])
-            hb = keep.tile([P, C, 4], BF16, name=f"hb{e}", align_bytes=64)
-            nc.scalar.activation(hb[:], turned[:].rearrange("p d u -> p u d"), ACT.Square)
-            h_bf[e] = hb
-
-        def quantise(e):
+            nc.scalar.activation(h_bf[e][:], turned[:].rearrange("p d u -> p u d"), ACT.Square)
             nc.vector.quantize_mx(
                 out=h_words[e][:].bitcast(FP8X4),
-                scales=h_scales[4 * e : P, :],
+                scales=h_scales[e][:],
                 in_=h_bf[e][:].rearrange("p u d -> p (u d)"),
             )
 
-        def second_layer(b, experts, engine):
+        def second_layer(b, experts, engine, n):
             c = [i for i, (b0, b1) in enumerate(W2_CUTS) if b0 <= b < b1][0]
             local = slice((b - W2_CUTS[c][0]) * P, (b - W2_CUTS[c][0] + 1) * P)
-            ysum = psum_y.tile([P, len(experts) * C], F32, name="ysum")
+            ysum = bank(n, [P, len(experts) * C])
             for i, e in enumerate(experts):
                 nc.tensor.matmul_mx(
                     out=ysum[:, i * C : (i + 1) * C],
                     lhsT=w2w[c][:, e, local].bitcast(FP8X4),
                     lhsT_scale=w2s[4 * e : P, b * P : (b + 1) * P],
                     rhs=h_words[e][:].bitcast(FP8X4),
-                    rhs_scale=h_scales[4 * e : P, :],
+                    rhs_scale=h_scales[e][:],
                     start=True,
                     stop=True,
                 )
@@ -194,85 +195,76 @@ def tile_moe_cpy_mlp_relu2_kernel(
             else:
                 nc.scalar.copy(dst, ysum[:])
 
-        def pick(b, r, lo, hi):
-            part = ring.tile([P, hi - lo], F32, name=f"part{r}", tag=f"part{r}")
+        def pick(b, r, lo, hi, tag):
+            part = keep.tile([P, hi - lo], F32, name=f"part{b}_{r}_{lo}", tag=tag)
             nc.vector.tensor_tensor(
-                part[:], ywin[b][:].indirect(pos_sb[r][:, lo // 16 : hi // 16]), gate_sb[:, r, lo:hi], ALU.mult
+                part[:], ywin[b][:].indirect(pos_sb[r][:, lo // 16 : hi // 16]), gate_sb[r][:, lo:hi], ALU.mult
             )
             return part
 
-        def add_on_tensor(b, parts):
-            res = ring.tile([P, T], F32, name="res")
-            for h in range(2):
-                by_token = psum.tile([P, 2, P], F32, name="by_token", tag="first")
-                for c in range(2):
-                    cols = slice(h * HALF + c * P, h * HALF + (c + 1) * P)
-                    for r in range(2):
-                        nc.tensor.matmul(
-                            by_token[:, c, :], parts[r][:, cols], ident[:],
-                            start=(r == 0), stop=(r == 1), is_transpose=True,
-                        )
-                summed = ring.tile([P, 2, P], F32, name="summed")
-                nc.scalar.copy(summed[:], by_token[:])
-                by_row = psum.tile([P, 2, P], F32, name="by_row", tag="second")
-                for c in range(2):
-                    nc.tensor.transpose(by_row[:, c, :], summed[:, c, :], ident[:])
-                nc.scalar.copy(res[:, h * HALF : (h + 1) * HALF], by_row[:].rearrange("p c t -> p (c t)"))
-            nc.sync.dma_start(out=out[b * P : (b + 1) * P, :], in_=res[:])
-
-        def add_on_vector(b, parts, lo, hi):
-            res = ring.tile([P, hi - lo], F32, name="res_v")
-            nc.vector.tensor_tensor(res[:], parts[0][:], parts[1][:], ALU.add)
+        def add_on_tensor(b, first, second, lo, hi, n):
+            chunks = (hi - lo) // P
+            by_token = bank(n, [P, chunks, P])
+            for c in range(chunks):
+                for r, part in enumerate((first, second)):
+                    nc.tensor.matmul(
+                        by_token[:, c, :], part[:, c * P : (c + 1) * P], ident[:],
+                        start=(r == 0), stop=(r == 1), is_transpose=True,
+                    )
+            summed = keep.tile([P, chunks, P], F32, name=f"summed{b}_{lo}", tag=f"summed{b}_{lo}")
+            nc.scalar.copy(summed[:], by_token[:])
+            by_row = bank(2 + n, [P, chunks, P])
+            for c in range(chunks):
+                nc.tensor.transpose(by_row[:, c, :], summed[:, c, :], ident[:])
+            res = keep.tile([P, hi - lo], F32, name=f"res{b}_{lo}")
+            nc.scalar.copy(res[:], by_row[:].rearrange("p c t -> p (c t)"))
             nc.sync.dma_start(out=out[b * P : (b + 1) * P, lo:hi], in_=res[:])
 
+        def add_on_vector(b, first, second, lo, hi, tag):
+            res = keep.tile([P, hi - lo], F32, name=f"res_v{b}_{lo}", tag=tag)
+            nc.vector.tensor_tensor(res[:], first, second, ALU.add)
+            nc.sync.dma_start(out=out[b * P : (b + 1) * P, lo:hi], in_=res[:])
+
+        idle = bank(7, [P, H])
         for i in range(WARM):
-            idle = psum_y.tile([P, 256], F32, name="ysum")
             nc.tensor.matmul_mx(
                 out=idle[:],
-                lhsT=w1w[0][:, 0, 0:P].bitcast(FP8X4),
-                lhsT_scale=w1s[0][:, 0:P],
-                rhs=w1w[0][:, 0, 0:256].bitcast(FP8X4),
-                rhs_scale=w1s[0][:, 0:256],
-                start=True,
-                stop=True,
+                lhsT=warm_words[:, 0:P].bitcast(FP8X4),
+                lhsT_scale=warm_scales[:, 0:P],
+                rhs=warm_words[:].bitcast(FP8X4),
+                rhs_scale=warm_scales[:],
+                start=(i == 0),
+                stop=(i == WARM - 1),
             )
-        gather_words(0, S // 2)
-        gather_words(S // 2, S)
-        gather_scales(*GATHER_CUTS[0])
-        first_layer(0)
-        gather_scales(*GATHER_CUTS[1])
-        first_layer(1)
-        gather_scales(*GATHER_CUTS[2])
-        square(0)
-        first_layer(2)
-        first_layer(3)
-        square(1)
-        square(2)
-        square(3)
         for e in range(E):
-            quantise(e)
-        second_layer(0, [0, 1], "scalar")
-        second_layer(0, [2, 3], "vector")
-        second_layer(1, [0, 1, 2, 3], "scalar")
-        waiting = None
-        for b in range(NB - 1):
-            first = pick(b, 0, 0, T)
-            if waiting is not None:
-                add_on_vector(b - 1, waiting, 0, T)
-                waiting = None
-            parts = [first, pick(b, 1, 0, T)]
-            if b + 2 < NB:
-                second_layer(b + 2, [0, 1, 2, 3], "scalar")
-            if b < PE_ADD_BLOCKS:
-                add_on_tensor(b, parts)
-            else:
-                waiting = parts
+            gather_slots(e)
+        first_layer(0, w1w[0], 0, H, 0)
+        first_layer(1, w1w[1], 0, H, 1)
+        square(0, 5)
+        first_layer(2, w1w[2], 0, H, 2)
+        square(1, 6)
+        first_layer(3, w1w_last[0], 0, HALF_H, 3)
+        square(2, 7)
+        first_layer(3, w1w_last[1], HALF_H, H, 4)
+        square(3, 5)
+        second_layer(0, [0, 1, 2], "scalar", 0)
+        second_layer(0, [3], "vector", 1)
+        for b, n in zip(range(1, NB), [2, 3, 4, 6, 7, 0, 1]):
+            second_layer(b, [0, 1, 2, 3], "scalar", n)
+        for b in range(NB - 2):
+            parts = [pick(b, r, 0, T, f"part{b}_{r}") for r in range(2)]
+            add_on_tensor(b, parts[0][:], parts[1][:], 0, T, b % 2)
+        b = NB - 2
+        first = pick(b, 0, 0, T, "first_6")
+        for h in range(2):
+            lo, hi = h * HALF_T, (h + 1) * HALF_T
+            second = pick(b, 1, lo, hi, f"second_6_{h}")
+            add_on_tensor(b, first[:, lo:hi], second[:], lo, hi, h)
         last = NB - 1
-        a0 = pick(last, 0, 0, HALF)
-        if waiting is not None:
-            add_on_vector(last - 1, waiting, 0, T)
-        b0 = pick(last, 1, 0, HALF)
-        a1 = pick(last, 0, HALF, T)
-        add_on_vector(last, [a0, b0], 0, HALF)
-        b1 = pick(last, 1, HALF, T)
-        add_on_vector(last, [a1, b1], HALF, T)
+        cut = T - TAIL
+        a0 = pick(last, 0, 0, cut, "a0")
+        b0 = pick(last, 1, 0, cut, "b0")
+        a1 = pick(last, 0, cut, T, "a1")
+        add_on_vector(last, a0[:], b0[:], 0, cut, f"summed{b}_0")
+        b1 = pick(last, 1, cut, T, "a0")
+        add_on_vector(last, a1[:], b1[:], cut, T, "res_tail")

@@ -24,6 +24,7 @@ HALF_H = H // 2
 HALF_T = T // 2
 TAIL = 128
 WARM = 4
+VECTOR_SUMS = (1, 3, 5)
 
 
 def tile_moe_cpy_mlp_relu2_kernel(
@@ -251,11 +252,21 @@ def tile_moe_cpy_mlp_relu2_kernel(
         second_layer(0, [3], "vector", 1)
         for b, n in zip(range(1, NB), [2, 3, 4, 6, 7, 0, 1]):
             second_layer(b, [0, 1, 2, 3], "scalar", n)
+        waiting = None
         for b in range(NB - 2):
-            parts = [pick(b, r, 0, T, f"part{b}_{r}") for r in range(2)]
-            add_on_tensor(b, parts[0][:], parts[1][:], 0, T, b % 2)
+            first = pick(b, 0, 0, T, f"part{b}_0")
+            if waiting is not None:
+                add_on_vector(b - 1, waiting[0][:], waiting[1][:], 0, T, f"res_v{b - 1}")
+                waiting = None
+            second = pick(b, 1, 0, T, f"part{b}_1")
+            if b in VECTOR_SUMS:
+                waiting = (first, second)
+            else:
+                add_on_tensor(b, first[:], second[:], 0, T, (b // 2) % 2)
         b = NB - 2
         first = pick(b, 0, 0, T, "first_6")
+        if waiting is not None:
+            add_on_vector(b - 1, waiting[0][:], waiting[1][:], 0, T, f"res_v{b - 1}")
         for h in range(2):
             lo, hi = h * HALF_T, (h + 1) * HALF_T
             second = pick(b, 1, lo, hi, f"second_6_{h}")

@@ -21,10 +21,9 @@ WIN = S + T + PAD
 NB = K // P
 W2_CUTS = [(0, 2), (2, 5), (5, 8)]
 HALF_H = H // 2
-HALF_T = T // 2
 TAIL = 128
 WARM = 4
-VECTOR_SUMS = (1, 3, 5)
+TENSOR_SUMS = 5
 
 
 def tile_moe_cpy_mlp_relu2_kernel(
@@ -118,9 +117,8 @@ def tile_moe_cpy_mlp_relu2_kernel(
             nc.sync.dma_start(out=gate_sb[r][:], in_=gate[r])
         load_xr(1)
         load_w2(1)
-        load_xr(2)
         load_w2(2)
-        for b in range(3, NB):
+        for b in range(2, NB):
             load_xr(b)
 
         for b in range(NB):
@@ -196,8 +194,8 @@ def tile_moe_cpy_mlp_relu2_kernel(
             else:
                 nc.scalar.copy(dst, ysum[:])
 
-        def pick(b, r, lo, hi, tag):
-            part = keep.tile([P, hi - lo], F32, name=f"part{b}_{r}_{lo}", tag=tag)
+        def pick(b, r, lo, hi):
+            part = keep.tile([P, hi - lo], F32, name=f"part{b}_{r}_{lo}")
             nc.vector.tensor_tensor(
                 part[:], ywin[b][:].indirect(pos_sb[r][:, lo // 16 : hi // 16]), gate_sb[r][:, lo:hi], ALU.mult
             )
@@ -212,17 +210,17 @@ def tile_moe_cpy_mlp_relu2_kernel(
                         by_token[:, c, :], part[:, c * P : (c + 1) * P], ident[:],
                         start=(r == 0), stop=(r == 1), is_transpose=True,
                     )
-            summed = keep.tile([P, chunks, P], F32, name=f"summed{b}_{lo}", tag=f"summed{b}_{lo}")
+            summed = keep.tile([P, chunks, P], F32, name=f"summed{b}_{lo}")
             nc.scalar.copy(summed[:], by_token[:])
             by_row = bank(2 + n, [P, chunks, P])
             for c in range(chunks):
                 nc.tensor.transpose(by_row[:, c, :], summed[:, c, :], ident[:])
             res = keep.tile([P, hi - lo], F32, name=f"res{b}_{lo}")
             nc.scalar.copy(res[:], by_row[:].rearrange("p c t -> p (c t)"))
-            nc.sync.dma_start(out=out[b * P : (b + 1) * P, lo:hi], in_=res[:])
+            nc.scalar.dma_start(out=out[b * P : (b + 1) * P, lo:hi], in_=res[:])
 
-        def add_on_vector(b, first, second, lo, hi, tag):
-            res = keep.tile([P, hi - lo], F32, name=f"res_v{b}_{lo}", tag=tag)
+        def add_on_vector(b, first, second, lo, hi):
+            res = keep.tile([P, hi - lo], F32, name=f"res_v{b}_{lo}")
             nc.vector.tensor_tensor(res[:], first, second, ALU.add)
             nc.sync.dma_start(out=out[b * P : (b + 1) * P, lo:hi], in_=res[:])
 
@@ -253,29 +251,22 @@ def tile_moe_cpy_mlp_relu2_kernel(
         for b, n in zip(range(1, NB), [2, 3, 4, 6, 7, 0, 1]):
             second_layer(b, [0, 1, 2, 3], "scalar", n)
         waiting = None
-        for b in range(NB - 2):
-            first = pick(b, 0, 0, T, f"part{b}_0")
+        for b in range(NB - 1):
+            first = pick(b, 0, 0, T)
             if waiting is not None:
-                add_on_vector(b - 1, waiting[0][:], waiting[1][:], 0, T, f"res_v{b - 1}")
+                add_on_vector(b - 1, waiting[0][:], waiting[1][:], 0, T)
                 waiting = None
-            second = pick(b, 1, 0, T, f"part{b}_1")
-            if b in VECTOR_SUMS:
-                waiting = (first, second)
+            second = pick(b, 1, 0, T)
+            if b < TENSOR_SUMS:
+                add_on_tensor(b, first[:], second[:], 0, T, b % 2)
             else:
-                add_on_tensor(b, first[:], second[:], 0, T, (b // 2) % 2)
-        b = NB - 2
-        first = pick(b, 0, 0, T, "first_6")
-        if waiting is not None:
-            add_on_vector(b - 1, waiting[0][:], waiting[1][:], 0, T, f"res_v{b - 1}")
-        for h in range(2):
-            lo, hi = h * HALF_T, (h + 1) * HALF_T
-            second = pick(b, 1, lo, hi, f"second_6_{h}")
-            add_on_tensor(b, first[:, lo:hi], second[:], lo, hi, h)
+                waiting = (first, second)
         last = NB - 1
         cut = T - TAIL
-        a0 = pick(last, 0, 0, cut, "a0")
-        b0 = pick(last, 1, 0, cut, "b0")
-        a1 = pick(last, 0, cut, T, "a1")
-        add_on_vector(last, a0[:], b0[:], 0, cut, f"summed{b}_0")
-        b1 = pick(last, 1, cut, T, "a0")
-        add_on_vector(last, a1[:], b1[:], cut, T, "res_tail")
+        a0 = pick(last, 0, 0, cut)
+        add_on_vector(last - 1, waiting[0][:], waiting[1][:], 0, T)
+        b0 = pick(last, 1, 0, cut)
+        a1 = pick(last, 0, cut, T)
+        add_on_vector(last, a0[:], b0[:], 0, cut)
+        b1 = pick(last, 1, cut, T)
+        add_on_vector(last, a1[:], b1[:], cut, T)

@@ -23,7 +23,7 @@ W2_CUTS = [(0, 2), (2, 5), (5, 8)]
 HALF_H = H // 2
 TAIL = 128
 WARM = 4
-TENSOR_SUMS = 5
+TENSOR_SUMS = 6
 
 
 def tile_moe_cpy_mlp_relu2_kernel(
@@ -41,8 +41,8 @@ def tile_moe_cpy_mlp_relu2_kernel(
         pos_sb = [keep.tile([P, T // 16], U16, name=f"pos_sb{r}") for r in range(2)]
         xw = keep.tile([P, 2 * T], U32, name="xw", align_bytes=64)
         xs = keep.tile([P, T], U8, name="xs", align_bytes=64)
-        w1w = [keep.tile([P, 2, H], U32, name=f"w1w{e}", align_bytes=64) for e in range(E - 1)]
-        w1w_last = [keep.tile([P, 2, HALF_H], U32, name=f"w1w_last{h}", align_bytes=64) for h in range(2)]
+        w1w = [keep.tile([P, 2, H], U32, name=f"w1w{e}", tag=f"w1w{e}", align_bytes=64) for e in range(E - 1)]
+        w1w_last = [keep.tile([P, 2, HALF_H], U32, name=f"w1w_last{h}", tag=f"w1w_last{h}", align_bytes=64) for h in range(2)]
         w1s = [keep.tile([P, H], U8, name=f"w1s{h}", align_bytes=64) for h in range(2)]
         w2w = [keep.tile([P, E, (b1 - b0) * P], U32, name=f"w2w{b0}", align_bytes=64) for b0, b1 in W2_CUTS]
         w2s = keep.tile([P, K], U8, name="w2s", align_bytes=64)
@@ -115,10 +115,8 @@ def tile_moe_cpy_mlp_relu2_kernel(
         for r, pos in enumerate((pos1, pos2)):
             nc.sync.dma_start(out=pos_sb[r][:], in_=pos)
             nc.sync.dma_start(out=gate_sb[r][:], in_=gate[r])
-        load_xr(1)
-        load_w2(1)
-        load_w2(2)
-        for b in range(2, NB):
+            load_w2(r + 1)
+        for b in range(1, NB):
             load_xr(b)
 
         for b in range(NB):
@@ -138,9 +136,10 @@ def tile_moe_cpy_mlp_relu2_kernel(
             nc.vector.tensor_copy(gs[:], xs[:].indirect(picks))
             slot_scales[e] = gs
 
-        h_words = [keep.tile([P, C], U32, name=f"h_words{e}", align_bytes=64) for e in range(E)]
+        h_words = {}
         h_scales = [keep.tile([P, C], U8, name=f"h_scales{e}", align_bytes=64) for e in range(E)]
-        relu_out = [keep.tile([P, 4, P], F32, name=f"relu_out{e}") for e in range(E)]
+        relu_out = {}
+        sums = {}
         h_bf = [keep.tile([P, C, 4], BF16, name=f"h_bf{e}", align_bytes=64) for e in range(E)]
 
         def first_layer(e, words, lo, hi, n):
@@ -156,7 +155,12 @@ def tile_moe_cpy_mlp_relu2_kernel(
                     start=(s == 0),
                     stop=(s == 1),
                 )
-            src = acc[:].rearrange("p (m d) -> p d m", d=4)
+            sums[e, lo] = acc
+
+        def relu(e, lo, hi, tag):
+            if e not in relu_out:
+                relu_out[e] = keep.tile([P, 4, P], F32, name=f"relu_out{e}", tag=tag, align_bytes=64)
+            src = sums[e, lo][:].rearrange("p (m d) -> p d m", d=4)
             dst = relu_out[e][:, :, lo // 4 : hi // 4]
             if e < 2:
                 nc.scalar.activation(dst, src, ACT.Relu)
@@ -168,8 +172,25 @@ def tile_moe_cpy_mlp_relu2_kernel(
             for d in range(4):
                 nc.tensor.transpose(turned[:, d, :], relu_out[e][:, d, :], ident[:])
             nc.scalar.activation(h_bf[e][:], turned[:].rearrange("p d u -> p u d"), ACT.Square)
+
+        def square_before_turning(e, n, tag):
+            kept = keep.tile([P, 2, P, 2], F32, name=f"kept{e}")
+            nc.scalar.activation(kept[:], sums[e, 0][:].rearrange("p (m u t) -> p u m t", u=2, t=2), ACT.Relu)
+            pairs = keep.tile([P, H], BF16, name=f"pairs{e}", tag=tag, align_bytes=64)
+            nc.scalar.activation(pairs[:], kept[:].rearrange("p u m t -> p (u m t)"), ACT.Square)
+            return pairs
+
+        def turn_pairs(e, pairs, n):
+            turned = bank(n, [P, 2, C])
+            words = pairs[:].bitcast(F32)
+            for u in range(2):
+                nc.tensor.transpose(turned[:, u, :], words[:, u * P : (u + 1) * P], ident[:])
+            dst = h_bf[e][:].rearrange("p s d -> p (s d)").bitcast(F32).rearrange("p (s u) -> p s u", u=2)
+            nc.vector.tensor_copy(dst, turned[:].rearrange("p u s -> p s u"))
+
+        def quantise(e):
             nc.vector.quantize_mx(
-                out=h_words[e][:].bitcast(FP8X4),
+                out=h_words[e].bitcast(FP8X4),
                 scales=h_scales[e][:],
                 in_=h_bf[e][:].rearrange("p u d -> p (u d)"),
             )
@@ -183,7 +204,7 @@ def tile_moe_cpy_mlp_relu2_kernel(
                     out=ysum[:, i * C : (i + 1) * C],
                     lhsT=w2w[c][:, e, local].bitcast(FP8X4),
                     lhsT_scale=w2s[4 * e : P, b * P : (b + 1) * P],
-                    rhs=h_words[e][:].bitcast(FP8X4),
+                    rhs=h_words[e].bitcast(FP8X4),
                     rhs_scale=h_scales[e][:],
                     start=True,
                     stop=True,
@@ -212,7 +233,7 @@ def tile_moe_cpy_mlp_relu2_kernel(
                     )
             summed = keep.tile([P, chunks, P], F32, name=f"summed{b}_{lo}")
             nc.scalar.copy(summed[:], by_token[:])
-            by_row = bank(2 + n, [P, chunks, P])
+            by_row = bank(3 + n, [P, chunks, P])
             for c in range(chunks):
                 nc.tensor.transpose(by_row[:, c, :], summed[:, c, :], ident[:])
             res = keep.tile([P, hi - lo], F32, name=f"res{b}_{lo}")
@@ -238,17 +259,27 @@ def tile_moe_cpy_mlp_relu2_kernel(
         for e in range(E):
             gather_slots(e)
         first_layer(0, w1w[0], 0, H, 0)
+        relu(0, 0, H, "relu0")
         first_layer(1, w1w[1], 0, H, 1)
         square(0, 5)
         first_layer(2, w1w[2], 0, H, 2)
-        square(1, 6)
+        pairs = square_before_turning(1, 6, "w1w2")
+        relu(2, 0, H, "relu2")
         first_layer(3, w1w_last[0], 0, HALF_H, 3)
-        square(2, 7)
+        relu(3, 0, HALF_H, "relu3")
         first_layer(3, w1w_last[1], HALF_H, H, 4)
+        relu(3, HALF_H, H, "relu3")
+        turn_pairs(1, pairs, 6)
+        square(2, 7)
         square(3, 5)
+        h_early = keep.tile([P, (E - 1) * C], U32, name="h_early", tag="w1w_last1", align_bytes=64)
+        h_late = keep.tile([P, C], U32, name="h_late", align_bytes=64)
+        for e in range(E):
+            h_words[e] = h_early[:, e * C : (e + 1) * C] if e < E - 1 else h_late[:]
+            quantise(e)
         second_layer(0, [0, 1, 2], "scalar", 0)
         second_layer(0, [3], "vector", 1)
-        for b, n in zip(range(1, NB), [2, 3, 4, 6, 7, 0, 1]):
+        for b, n in zip([1, 2, 5, 3, 4, 6, 7], [2, 3, 0, 4, 6, 1, 7]):
             second_layer(b, [0, 1, 2, 3], "scalar", n)
         waiting = None
         for b in range(NB - 1):
@@ -257,8 +288,12 @@ def tile_moe_cpy_mlp_relu2_kernel(
                 add_on_vector(b - 1, waiting[0][:], waiting[1][:], 0, T)
                 waiting = None
             second = pick(b, 1, 0, T)
-            if b < TENSOR_SUMS:
+            if b < TENSOR_SUMS - 1:
                 add_on_tensor(b, first[:], second[:], 0, T, b % 2)
+            elif b < TENSOR_SUMS:
+                for h in range(2):
+                    cols = slice(h * T // 2, (h + 1) * T // 2)
+                    add_on_tensor(b, first[:, cols], second[:, cols], cols.start, cols.stop, (b + h) % 2)
             else:
                 waiting = (first, second)
         last = NB - 1

@@ -23,7 +23,7 @@ W2_CUTS = [(0, 2), (2, 5), (5, 8)]
 HALF_H = H // 2
 TAIL = 128
 WARM = 4
-TENSOR_SUMS = 6
+TENSOR_SUMS = 5
 
 
 def tile_moe_cpy_mlp_relu2_kernel(
@@ -51,8 +51,8 @@ def tile_moe_cpy_mlp_relu2_kernel(
         zeros = keep.tile([P, PAD], F32, name="zeros")
         ident = keep.tile([P, P], F32, name="ident")
 
-        nc.gpsimd.memset(w1s[0][:].bitcast(I32), 0)
-        for plane in (xs, w1s[1], w2s):
+        nc.gpsimd.memset(xs[:].bitcast(I32), 0)
+        for plane in (w1s[0], w1s[1], w2s):
             nc.vector.memset(plane[:].bitcast(I32), 0)
         nc.vector.memset(zeros[:], 0.0)
         warm_in = keep.tile([P, 4 * H], BF16, name="warm_in", align_bytes=64)
@@ -93,30 +93,35 @@ def tile_moe_cpy_mlp_relu2_kernel(
             nc.scalar.activation(ywin[b][:, S + T : WIN], zeros[:], ACT.Square)
 
         w1_rows = w1_scales.rearrange("e s b i -> (e s) b i")
+        def load_w1(e):
+            nc.sync.dma_start(out=w1w[e][:].bitcast(I32), in_=w1_src[e])
+
         nc.sync.dma_start(out=offs_sb[:], in_=offs)
-        load_planes(nc.sync, w1s[0], w1_rows[0:4], range(2))
         load_planes(nc.sync, xs, x_scales, range(4))
         nc.sync.dma_start(
             out=xw[:].bitcast(I32).rearrange("p (s t) -> p s t", s=2),
             in_=x_words.rearrange("s p t d -> p s (t d)").bitcast(I32),
         )
-        load_planes(nc.sync, w1s[0], w1_rows[0:4], range(2, 4))
-        for e in range(E - 1):
-            if e == 2:
-                load_planes(nc.sync, w1s[1], w1_rows[4:8], range(4))
-            nc.sync.dma_start(out=w1w[e][:].bitcast(I32), in_=w1_src[e])
+        load_w1(0)
+        load_planes(nc.sync, w1s[0], w1_rows[0:4], range(4))
+        load_w1(1)
+        load_w1(2)
+        load_planes(nc.sync, w1s[1], w1_rows[4:8], range(4))
         for h in range(2):
             nc.sync.dma_start(
                 out=w1w_last[h][:].bitcast(I32), in_=w1_src[E - 1][:, :, h * HALF_H : (h + 1) * HALF_H]
             )
-        load_planes(nc.sync, w2s, w2_scales.rearrange("e s b n -> (e s) b n"), range(4))
         load_w2(0)
         load_xr(0)
-        for r, pos in enumerate((pos1, pos2)):
-            nc.sync.dma_start(out=pos_sb[r][:], in_=pos)
-            nc.sync.dma_start(out=gate_sb[r][:], in_=gate[r])
-            load_w2(r + 1)
-        for b in range(1, NB):
+        load_planes(nc.sync, w2s, w2_scales.rearrange("e s b n -> (e s) b n"), range(4))
+        nc.sync.dma_start(out=gate_sb[0][:], in_=gate[0])
+        nc.sync.dma_start(out=pos_sb[0][:], in_=pos1)
+        nc.sync.dma_start(out=gate_sb[1][:], in_=gate[1])
+        load_xr(1)
+        nc.sync.dma_start(out=pos_sb[1][:], in_=pos2)
+        load_w2(1)
+        load_w2(2)
+        for b in range(2, NB):
             load_xr(b)
 
         for b in range(NB):
@@ -162,7 +167,7 @@ def tile_moe_cpy_mlp_relu2_kernel(
                 relu_out[e] = keep.tile([P, 4, P], F32, name=f"relu_out{e}", tag=tag, align_bytes=64)
             src = sums[e, lo][:].rearrange("p (m d) -> p d m", d=4)
             dst = relu_out[e][:, :, lo // 4 : hi // 4]
-            if e < 2:
+            if e == 0 or (e == E - 1 and lo == 0):
                 nc.scalar.activation(dst, src, ACT.Relu)
             else:
                 nc.vector.tensor_scalar_max(dst, src, 0.0)
@@ -269,8 +274,8 @@ def tile_moe_cpy_mlp_relu2_kernel(
         relu(3, 0, HALF_H, "relu3")
         first_layer(3, w1w_last[1], HALF_H, H, 4)
         relu(3, HALF_H, H, "relu3")
-        turn_pairs(1, pairs, 6)
         square(2, 7)
+        turn_pairs(1, pairs, 6)
         square(3, 5)
         h_early = keep.tile([P, (E - 1) * C], U32, name="h_early", tag="w1w_last1", align_bytes=64)
         h_late = keep.tile([P, C], U32, name="h_late", align_bytes=64)
@@ -288,12 +293,8 @@ def tile_moe_cpy_mlp_relu2_kernel(
                 add_on_vector(b - 1, waiting[0][:], waiting[1][:], 0, T)
                 waiting = None
             second = pick(b, 1, 0, T)
-            if b < TENSOR_SUMS - 1:
+            if b < TENSOR_SUMS:
                 add_on_tensor(b, first[:], second[:], 0, T, b % 2)
-            elif b < TENSOR_SUMS:
-                for h in range(2):
-                    cols = slice(h * T // 2, (h + 1) * T // 2)
-                    add_on_tensor(b, first[:, cols], second[:, cols], cols.start, cols.stop, (b + h) % 2)
             else:
                 waiting = (first, second)
         last = NB - 1

@@ -16,14 +16,14 @@ ACT = mybir.ActivationFunctionType
 ALU = mybir.AluOpType
 
 P = 128
-S = E * C
-WIN = S + T + PAD
-NB = K // P
-W2_CUTS = [(0, 2), (2, 5), (5, 8)]
+SLOTS = E * C
+WINDOW = SLOTS + T + PAD
+ROW_BLOCKS = K // P
+LAST_EXPERT = E - 1
 HALF_H = H // 2
-TAIL = 128
-WARM = 4
+W2_PIECES = [(0, 2), (2, 5), (5, 8)]
 TENSOR_SUMS = 5
+TAIL = 128
 
 
 def tile_moe_cpy_mlp_relu2_kernel(
@@ -37,29 +37,27 @@ def tile_moe_cpy_mlp_relu2_kernel(
         def bank(n, shape):
             return psum.tile(shape, F32, name=f"bank{n}", tag=f"bank{n}")
 
-        offs_sb = keep.tile([P, S // 16], U16, name="offs_sb")
+        offs_sb = keep.tile([P, SLOTS // 16], U16, name="offs_sb")
         pos_sb = [keep.tile([P, T // 16], U16, name=f"pos_sb{r}") for r in range(2)]
         xw = keep.tile([P, 2 * T], U32, name="xw", align_bytes=64)
         xs = keep.tile([P, T], U8, name="xs", align_bytes=64)
-        w1w = [keep.tile([P, 2, H], U32, name=f"w1w{e}", tag=f"w1w{e}", align_bytes=64) for e in range(E - 1)]
-        w1w_last = [keep.tile([P, 2, HALF_H], U32, name=f"w1w_last{h}", tag=f"w1w_last{h}", align_bytes=64) for h in range(2)]
-        w1s = [keep.tile([P, H], U8, name=f"w1s{h}", align_bytes=64) for h in range(2)]
-        w2w = [keep.tile([P, E, (b1 - b0) * P], U32, name=f"w2w{b0}", align_bytes=64) for b0, b1 in W2_CUTS]
+        w1w = [keep.tile([P, 2, H], U32, name=f"w1w{e}", tag=f"w1w{e}", align_bytes=64) for e in range(LAST_EXPERT)]
+        w1w_last = [
+            keep.tile([P, 2, HALF_H], U32, name=f"w1w_last{h}", tag=f"w1w_last{h}", align_bytes=64) for h in range(2)
+        ]
+        w1s = [keep.tile([P, H], U8, name=f"w1s{j}", align_bytes=64) for j in range(2)]
+        w2w = [keep.tile([P, E, (b1 - b0) * P], U32, name=f"w2w{b0}", align_bytes=64) for b0, b1 in W2_PIECES]
         w2s = keep.tile([P, K], U8, name="w2s", align_bytes=64)
         gate_sb = [keep.tile([P, T], F32, name=f"gate_sb{r}") for r in range(2)]
-        ywin = [keep.tile([P, WIN], F32, name=f"ywin{b}") for b in range(NB)]
+        window = [keep.tile([P, WINDOW], F32, name=f"window{b}") for b in range(ROW_BLOCKS)]
         zeros = keep.tile([P, PAD], F32, name="zeros")
         ident = keep.tile([P, P], F32, name="ident")
 
-        nc.gpsimd.memset(xs[:].bitcast(I32), 0)
-        for plane in (w1s[0], w1s[1], w2s):
-            nc.vector.memset(plane[:].bitcast(I32), 0)
+        nc.gpsimd.memset(w1s[0][:].bitcast(I32), 0)
+        for scales in (xs, w1s[1], w2s):
+            nc.vector.memset(scales[:].bitcast(I32), 0)
         nc.vector.memset(zeros[:], 0.0)
-        warm_in = keep.tile([P, 4 * H], BF16, name="warm_in", align_bytes=64)
-        warm_words = keep.tile([P, H], U32, name="warm_words", align_bytes=64)
-        warm_scales = keep.tile([P, H], U8, name="warm_scales", align_bytes=64)
-        nc.gpsimd.memset(warm_in[:].bitcast(I32), 0)
-        nc.vector.quantize_mx(out=warm_words[:].bitcast(FP8X4), scales=warm_scales[:], in_=warm_in[:])
+
         ones = keep.tile([P, 32], F32, name="ones")
         column = keep.tile([P, 32], F32, name="column", align_bytes=64)
         row = keep.tile([P, 32], F32, name="row", align_bytes=64)
@@ -73,59 +71,56 @@ def tile_moe_cpy_mlp_relu2_kernel(
 
         w1_src = w1_words.rearrange("e s p i d -> e p s (i d)").bitcast(I32)
         w2_src = w2_words.rearrange("e s p n d -> p (e s) (n d)").bitcast(I32)
+        w1_passes = w1_scales.rearrange("e s b i -> (e s) b i")
 
-        def load_w2(c):
-            b0, b1 = W2_CUTS[c]
-            nc.sync.dma_start(out=w2w[c][:].bitcast(I32), in_=w2_src[:, :, b0 * P : b1 * P])
-
-        def load_xr(b):
-            nc.sync.dma_start(out=ywin[b][:, S : S + T], in_=xr[b * P : (b + 1) * P, :])
-
-        def load_planes(queue, plane, rows, quadrants):
-            count = rows.shape[0]
-            for q in quadrants:
-                queue.dma_start(
-                    out=plane[32 * q : 32 * q + 4 * count, :].bitcast(I32),
-                    in_=rows[:, 4 * q : 4 * q + 4, :].bitcast(I32),
-                )
-
-        def clear_zero_expert(b):
-            nc.scalar.activation(ywin[b][:, S + T : WIN], zeros[:], ACT.Square)
-
-        w1_rows = w1_scales.rearrange("e s b i -> (e s) b i")
         def load_w1(e):
             nc.sync.dma_start(out=w1w[e][:].bitcast(I32), in_=w1_src[e])
 
+        def load_w2(piece):
+            b0, b1 = W2_PIECES[piece]
+            nc.sync.dma_start(out=w2w[piece][:].bitcast(I32), in_=w2_src[:, :, b0 * P : b1 * P])
+
+        def load_xr(b):
+            nc.sync.dma_start(out=window[b][:, SLOTS : SLOTS + T], in_=xr[b * P : (b + 1) * P, :])
+
+        def load_scales(scales, passes, quadrants):
+            count = passes.shape[0]
+            for q in quadrants:
+                nc.sync.dma_start(
+                    out=scales[32 * q : 32 * q + 4 * count, :].bitcast(I32),
+                    in_=passes[:, 4 * q : 4 * q + 4, :].bitcast(I32),
+                )
+
         nc.sync.dma_start(out=offs_sb[:], in_=offs)
-        load_planes(nc.sync, xs, x_scales, range(4))
+        load_scales(w1s[0], w1_passes[0:4], range(2))
+        load_scales(xs, x_scales, range(4))
         nc.sync.dma_start(
             out=xw[:].bitcast(I32).rearrange("p (s t) -> p s t", s=2),
             in_=x_words.rearrange("s p t d -> p s (t d)").bitcast(I32),
         )
+        load_scales(w1s[0], w1_passes[0:4], range(2, 4))
         load_w1(0)
-        load_planes(nc.sync, w1s[0], w1_rows[0:4], range(4))
         load_w1(1)
+        load_scales(w1s[1], w1_passes[4:8], range(4))
         load_w1(2)
-        load_planes(nc.sync, w1s[1], w1_rows[4:8], range(4))
         for h in range(2):
             nc.sync.dma_start(
-                out=w1w_last[h][:].bitcast(I32), in_=w1_src[E - 1][:, :, h * HALF_H : (h + 1) * HALF_H]
+                out=w1w_last[h][:].bitcast(I32), in_=w1_src[LAST_EXPERT][:, :, h * HALF_H : (h + 1) * HALF_H]
             )
+        load_scales(w2s, w2_scales.rearrange("e s b n -> (e s) b n"), range(4))
         load_w2(0)
         load_xr(0)
-        load_planes(nc.sync, w2s, w2_scales.rearrange("e s b n -> (e s) b n"), range(4))
-        nc.sync.dma_start(out=gate_sb[0][:], in_=gate[0])
-        nc.sync.dma_start(out=pos_sb[0][:], in_=pos1)
-        nc.sync.dma_start(out=gate_sb[1][:], in_=gate[1])
+        for r, pos in enumerate((pos1, pos2)):
+            nc.sync.dma_start(out=pos_sb[r][:], in_=pos)
+            nc.sync.dma_start(out=gate_sb[r][:], in_=gate[r])
         load_xr(1)
-        nc.sync.dma_start(out=pos_sb[1][:], in_=pos2)
         load_w2(1)
         load_w2(2)
-        for b in range(2, NB):
+        for b in range(2, ROW_BLOCKS):
             load_xr(b)
 
-        for b in range(NB):
-            clear_zero_expert(b)
+        for b in range(ROW_BLOCKS):
+            nc.scalar.activation(window[b][:, SLOTS + T : WINDOW], zeros[:], ACT.Square)
 
         slot_words = {}
         slot_scales = {}
@@ -134,175 +129,159 @@ def tile_moe_cpy_mlp_relu2_kernel(
             picks = offs_sb[:, e * C // 16 : (e + 1) * C // 16]
             slot_words[e] = []
             for s in range(2):
-                g = keep.tile([P, C], U32, name=f"xg{e}_{s}", align_bytes=64)
-                nc.vector.tensor_copy(g[:], xw[:, s * T : (s + 1) * T].indirect(picks))
-                slot_words[e].append(g)
-            gs = keep.tile([P, C], U8, name=f"xgs{e}", align_bytes=64)
-            nc.vector.tensor_copy(gs[:], xs[:].indirect(picks))
-            slot_scales[e] = gs
+                words = keep.tile([P, C], U32, name=f"slot_words{e}_{s}", align_bytes=64)
+                nc.vector.tensor_copy(words[:], xw[:, s * T : (s + 1) * T].indirect(picks))
+                slot_words[e].append(words)
+            slot_scales[e] = keep.tile([P, C], U8, name=f"slot_scales{e}", align_bytes=64)
+            nc.vector.tensor_copy(slot_scales[e][:], xs[:].indirect(picks))
 
         h_words = {}
         h_scales = [keep.tile([P, C], U8, name=f"h_scales{e}", align_bytes=64) for e in range(E)]
-        relu_out = {}
-        sums = {}
         h_bf = [keep.tile([P, C, 4], BF16, name=f"h_bf{e}", align_bytes=64) for e in range(E)]
 
         def first_layer(e, words, lo, hi, n):
-            acc = bank(n, [P, hi - lo])
+            sums = bank(n, [P, hi - lo])
             for s in range(2):
-                j = 2 * (e % 2) + s
+                place = 2 * (e % 2) + s
                 nc.tensor.matmul_mx(
-                    out=acc[:],
+                    out=sums[:],
                     lhsT=slot_words[e][s][:].bitcast(FP8X4),
                     lhsT_scale=slot_scales[e][4 * s : P, :],
                     rhs=words[:, s, :].bitcast(FP8X4),
-                    rhs_scale=w1s[e // 2][4 * j : P, lo:hi],
+                    rhs_scale=w1s[e // 2][4 * place : P, lo:hi],
                     start=(s == 0),
                     stop=(s == 1),
                 )
-            sums[e, lo] = acc
+            return sums
 
-        def relu(e, lo, hi, tag):
-            if e not in relu_out:
-                relu_out[e] = keep.tile([P, 4, P], F32, name=f"relu_out{e}", tag=tag, align_bytes=64)
-            src = sums[e, lo][:].rearrange("p (m d) -> p d m", d=4)
-            dst = relu_out[e][:, :, lo // 4 : hi // 4]
-            if e == 0 or (e == E - 1 and lo == 0):
-                nc.scalar.activation(dst, src, ACT.Relu)
-            else:
-                nc.vector.tensor_scalar_max(dst, src, 0.0)
+        def by_byte(sums):
+            return sums[:].rearrange("p (m d) -> p d m", d=4)
 
-        def square(e, n):
+        def relu_tile(e):
+            return keep.tile([P, 4, P], F32, name=f"relu{e}", align_bytes=64)
+
+        def turn_and_square(e, relu, n):
             turned = bank(n, [P, 4, C])
             for d in range(4):
-                nc.tensor.transpose(turned[:, d, :], relu_out[e][:, d, :], ident[:])
-            nc.scalar.activation(h_bf[e][:], turned[:].rearrange("p d u -> p u d"), ACT.Square)
+                nc.tensor.transpose(turned[:, d, :], relu[:, d, :], ident[:])
+            nc.scalar.activation(h_bf[e][:], turned[:].rearrange("p d c -> p c d"), ACT.Square)
 
-        def square_before_turning(e, n, tag):
-            kept = keep.tile([P, 2, P, 2], F32, name=f"kept{e}")
-            nc.scalar.activation(kept[:], sums[e, 0][:].rearrange("p (m u t) -> p u m t", u=2, t=2), ACT.Relu)
-            pairs = keep.tile([P, H], BF16, name=f"pairs{e}", tag=tag, align_bytes=64)
-            nc.scalar.activation(pairs[:], kept[:].rearrange("p u m t -> p (u m t)"), ACT.Square)
+        def square_into_pairs(sums, tag):
+            relu = keep.tile([P, 2, P, 2], F32, name="relu_pairs")
+            nc.scalar.activation(relu[:], sums[:].rearrange("p (m u t) -> p u m t", u=2, t=2), ACT.Relu)
+            pairs = keep.tile([P, H], BF16, name="pairs", tag=tag, align_bytes=64)
+            nc.scalar.activation(pairs[:], relu[:].rearrange("p u m t -> p (u m t)"), ACT.Square)
             return pairs
 
         def turn_pairs(e, pairs, n):
             turned = bank(n, [P, 2, C])
-            words = pairs[:].bitcast(F32)
+            as_f32 = pairs[:].bitcast(F32)
             for u in range(2):
-                nc.tensor.transpose(turned[:, u, :], words[:, u * P : (u + 1) * P], ident[:])
-            dst = h_bf[e][:].rearrange("p s d -> p (s d)").bitcast(F32).rearrange("p (s u) -> p s u", u=2)
-            nc.vector.tensor_copy(dst, turned[:].rearrange("p u s -> p s u"))
+                nc.tensor.transpose(turned[:, u, :], as_f32[:, u * P : (u + 1) * P], ident[:])
+            dst = h_bf[e][:].rearrange("p c d -> p (c d)").bitcast(F32).rearrange("p (c u) -> p c u", u=2)
+            nc.vector.tensor_copy(dst, turned[:].rearrange("p u c -> p c u"))
 
-        def quantise(e):
-            nc.vector.quantize_mx(
-                out=h_words[e].bitcast(FP8X4),
-                scales=h_scales[e][:],
-                in_=h_bf[e][:].rearrange("p u d -> p (u d)"),
-            )
-
-        def second_layer(b, experts, engine, n):
-            c = [i for i, (b0, b1) in enumerate(W2_CUTS) if b0 <= b < b1][0]
-            local = slice((b - W2_CUTS[c][0]) * P, (b - W2_CUTS[c][0] + 1) * P)
-            ysum = bank(n, [P, len(experts) * C])
+        def second_layer(b, experts, n):
+            piece = [i for i, (b0, b1) in enumerate(W2_PIECES) if b0 <= b < b1][0]
+            local = b - W2_PIECES[piece][0]
+            y = bank(n, [P, len(experts) * C])
             for i, e in enumerate(experts):
                 nc.tensor.matmul_mx(
-                    out=ysum[:, i * C : (i + 1) * C],
-                    lhsT=w2w[c][:, e, local].bitcast(FP8X4),
+                    out=y[:, i * C : (i + 1) * C],
+                    lhsT=w2w[piece][:, e, local * P : (local + 1) * P].bitcast(FP8X4),
                     lhsT_scale=w2s[4 * e : P, b * P : (b + 1) * P],
                     rhs=h_words[e].bitcast(FP8X4),
                     rhs_scale=h_scales[e][:],
                     start=True,
                     stop=True,
                 )
-            dst = ywin[b][:, experts[0] * C : (experts[-1] + 1) * C]
-            if engine == "vector":
-                nc.vector.tensor_copy(dst, ysum[:])
-            else:
-                nc.scalar.copy(dst, ysum[:])
+            return window[b][:, experts[0] * C : (experts[-1] + 1) * C], y[:]
 
         def pick(b, r, lo, hi):
-            part = keep.tile([P, hi - lo], F32, name=f"part{b}_{r}_{lo}")
+            product = keep.tile([P, hi - lo], F32, name=f"product{b}_{r}_{lo}")
             nc.vector.tensor_tensor(
-                part[:], ywin[b][:].indirect(pos_sb[r][:, lo // 16 : hi // 16]), gate_sb[r][:, lo:hi], ALU.mult
+                product[:], window[b][:].indirect(pos_sb[r][:, lo // 16 : hi // 16]), gate_sb[r][:, lo:hi], ALU.mult
             )
-            return part
+            return product
 
-        def add_on_tensor(b, first, second, lo, hi, n):
-            chunks = (hi - lo) // P
-            by_token = bank(n, [P, chunks, P])
-            for c in range(chunks):
-                for r, part in enumerate((first, second)):
+        def add_on_tensor(b, first, second):
+            by_token = bank(b % 2, [P, T // P, P])
+            for c in range(T // P):
+                for r, product in enumerate((first, second)):
                     nc.tensor.matmul(
-                        by_token[:, c, :], part[:, c * P : (c + 1) * P], ident[:],
+                        by_token[:, c, :], product[:, c * P : (c + 1) * P], ident[:],
                         start=(r == 0), stop=(r == 1), is_transpose=True,
                     )
-            summed = keep.tile([P, chunks, P], F32, name=f"summed{b}_{lo}")
+            summed = keep.tile([P, T // P, P], F32, name=f"summed{b}")
             nc.scalar.copy(summed[:], by_token[:])
-            by_row = bank(3 + n, [P, chunks, P])
-            for c in range(chunks):
+            by_row = bank(3 + b % 2, [P, T // P, P])
+            for c in range(T // P):
                 nc.tensor.transpose(by_row[:, c, :], summed[:, c, :], ident[:])
-            res = keep.tile([P, hi - lo], F32, name=f"res{b}_{lo}")
-            nc.scalar.copy(res[:], by_row[:].rearrange("p c t -> p (c t)"))
-            nc.scalar.dma_start(out=out[b * P : (b + 1) * P, lo:hi], in_=res[:])
+            result = keep.tile([P, T], F32, name=f"result{b}")
+            nc.scalar.copy(result[:], by_row[:].rearrange("p c t -> p (c t)"))
+            nc.scalar.dma_start(out=out[b * P : (b + 1) * P, :], in_=result[:])
 
         def add_on_vector(b, first, second, lo, hi):
-            res = keep.tile([P, hi - lo], F32, name=f"res_v{b}_{lo}")
-            nc.vector.tensor_tensor(res[:], first, second, ALU.add)
-            nc.sync.dma_start(out=out[b * P : (b + 1) * P, lo:hi], in_=res[:])
+            result = keep.tile([P, hi - lo], F32, name=f"result{b}_{lo}")
+            nc.vector.tensor_tensor(result[:], first[:], second[:], ALU.add)
+            nc.sync.dma_start(out=out[b * P : (b + 1) * P, lo:hi], in_=result[:])
 
-        idle = bank(7, [P, H])
-        for i in range(WARM):
-            nc.tensor.matmul_mx(
-                out=idle[:],
-                lhsT=warm_words[:, 0:P].bitcast(FP8X4),
-                lhsT_scale=warm_scales[:, 0:P],
-                rhs=warm_words[:].bitcast(FP8X4),
-                rhs_scale=warm_scales[:],
-                start=(i == 0),
-                stop=(i == WARM - 1),
-            )
         for e in range(E):
             gather_slots(e)
-        first_layer(0, w1w[0], 0, H, 0)
-        relu(0, 0, H, "relu0")
-        first_layer(1, w1w[1], 0, H, 1)
-        square(0, 5)
-        first_layer(2, w1w[2], 0, H, 2)
-        pairs = square_before_turning(1, 6, "w1w2")
-        relu(2, 0, H, "relu2")
-        first_layer(3, w1w_last[0], 0, HALF_H, 3)
-        relu(3, 0, HALF_H, "relu3")
-        first_layer(3, w1w_last[1], HALF_H, H, 4)
-        relu(3, HALF_H, H, "relu3")
-        square(2, 7)
-        turn_pairs(1, pairs, 6)
-        square(3, 5)
-        h_early = keep.tile([P, (E - 1) * C], U32, name="h_early", tag="w1w_last1", align_bytes=64)
+
+        sums0 = first_layer(0, w1w[0], 0, H, 0)
+        relu0 = relu_tile(0)
+        nc.scalar.activation(relu0[:], by_byte(sums0), ACT.Relu)
+        sums1 = first_layer(1, w1w[1], 0, H, 1)
+        turn_and_square(0, relu0, 5)
+        sums2 = first_layer(2, w1w[2], 0, H, 2)
+        pairs1 = square_into_pairs(sums1, "w1w2")
+        relu2 = relu_tile(2)
+        nc.vector.tensor_scalar_max(relu2[:], by_byte(sums2), 0.0)
+        sums3a = first_layer(LAST_EXPERT, w1w_last[0], 0, HALF_H, 3)
+        relu3 = relu_tile(LAST_EXPERT)
+        nc.scalar.activation(relu3[:, :, 0 : P // 2], by_byte(sums3a), ACT.Relu)
+        sums3b = first_layer(LAST_EXPERT, w1w_last[1], HALF_H, H, 4)
+        nc.vector.tensor_scalar_max(relu3[:, :, P // 2 : P], by_byte(sums3b), 0.0)
+        turn_and_square(2, relu2, 7)
+        turn_pairs(1, pairs1, 6)
+        turn_and_square(LAST_EXPERT, relu3, 5)
+
+        h_early = keep.tile([P, LAST_EXPERT * C], U32, name="h_early", tag="w1w_last1", align_bytes=64)
         h_late = keep.tile([P, C], U32, name="h_late", align_bytes=64)
         for e in range(E):
-            h_words[e] = h_early[:, e * C : (e + 1) * C] if e < E - 1 else h_late[:]
-            quantise(e)
-        second_layer(0, [0, 1, 2], "scalar", 0)
-        second_layer(0, [3], "vector", 1)
-        for b, n in zip([1, 2, 5, 3, 4, 6, 7], [2, 3, 0, 4, 6, 1, 7]):
-            second_layer(b, [0, 1, 2, 3], "scalar", n)
+            h_words[e] = h_early[:, e * C : (e + 1) * C] if e < LAST_EXPERT else h_late[:]
+            nc.vector.quantize_mx(
+                out=h_words[e].bitcast(FP8X4),
+                scales=h_scales[e][:],
+                in_=h_bf[e][:].rearrange("p c d -> p (c d)"),
+            )
+
+        nc.scalar.copy(*second_layer(0, list(range(LAST_EXPERT)), 0))
+        nc.vector.tensor_copy(*second_layer(0, [LAST_EXPERT], 1))
+        held = W2_PIECES[-1][0]
+        order = [1, 2, held] + [b for b in range(3, ROW_BLOCKS) if b != held]
+        others = [b for b in order if b not in (held, held + 1)]
+        bank_of = dict(zip([held, held + 1] + others, [0, 1, 2, 3, 4, 6, 7]))
+        for b in order:
+            nc.scalar.copy(*second_layer(b, list(range(E)), bank_of[b]))
+
         waiting = None
-        for b in range(NB - 1):
+        for b in range(ROW_BLOCKS - 1):
             first = pick(b, 0, 0, T)
             if waiting is not None:
-                add_on_vector(b - 1, waiting[0][:], waiting[1][:], 0, T)
-                waiting = None
+                add_on_vector(b - 1, *waiting, 0, T)
             second = pick(b, 1, 0, T)
             if b < TENSOR_SUMS:
-                add_on_tensor(b, first[:], second[:], 0, T, b % 2)
+                add_on_tensor(b, first, second)
             else:
                 waiting = (first, second)
-        last = NB - 1
+        last = ROW_BLOCKS - 1
         cut = T - TAIL
-        a0 = pick(last, 0, 0, cut)
-        add_on_vector(last - 1, waiting[0][:], waiting[1][:], 0, T)
-        b0 = pick(last, 1, 0, cut)
-        a1 = pick(last, 0, cut, T)
-        add_on_vector(last, a0[:], b0[:], 0, cut)
-        b1 = pick(last, 1, cut, T)
-        add_on_vector(last, a1[:], b1[:], cut, T)
+        head_first = pick(last, 0, 0, cut)
+        add_on_vector(last - 1, *waiting, 0, T)
+        head_second = pick(last, 1, 0, cut)
+        tail_first = pick(last, 0, cut, T)
+        add_on_vector(last, head_first, head_second, 0, cut)
+        tail_second = pick(last, 1, cut, T)
+        add_on_vector(last, tail_first, tail_second, cut, T)

@@ -22,7 +22,7 @@ ROW_BLOCKS = K // P
 LAST_EXPERT = E - 1
 HALF_H = H // 2
 W2_PIECES = [(0, 2), (2, 5), (5, 8)]
-TENSOR_SUMS = 5
+TENSOR_SUMS = 6
 TAIL = 128
 
 
@@ -204,8 +204,8 @@ def tile_moe_cpy_mlp_relu2_kernel(
             )
             return product
 
-        def add_on_tensor(b, first, second):
-            by_token = bank(b % 2, [P, T // P, P])
+        def sum_by_token(b, first, second, n):
+            by_token = bank(n, [P, T // P, P])
             for c in range(T // P):
                 for r, product in enumerate((first, second)):
                     nc.tensor.matmul(
@@ -214,7 +214,10 @@ def tile_moe_cpy_mlp_relu2_kernel(
                     )
             summed = keep.tile([P, T // P, P], F32, name=f"summed{b}")
             nc.scalar.copy(summed[:], by_token[:])
-            by_row = bank(3 + b % 2, [P, T // P, P])
+            return summed
+
+        def turn_back(b, summed, n):
+            by_row = bank(n, [P, T // P, P])
             for c in range(T // P):
                 nc.tensor.transpose(by_row[:, c, :], summed[:, c, :], ident[:])
             result = keep.tile([P, T], F32, name=f"result{b}")
@@ -259,23 +262,36 @@ def tile_moe_cpy_mlp_relu2_kernel(
 
         nc.scalar.copy(*second_layer(0, list(range(LAST_EXPERT)), 0))
         nc.vector.tensor_copy(*second_layer(0, [LAST_EXPERT], 1))
-        held = W2_PIECES[-1][0]
-        order = [1, 2, held] + [b for b in range(3, ROW_BLOCKS) if b != held]
-        others = [b for b in order if b not in (held, held + 1)]
-        bank_of = dict(zip([held, held + 1] + others, [0, 1, 2, 3, 4, 6, 7]))
-        for b in order:
-            nc.scalar.copy(*second_layer(b, list(range(E)), bank_of[b]))
+
+        def fill_window(b, n):
+            nc.scalar.copy(*second_layer(b, list(range(E)), n))
+
+        def both(b):
+            return pick(b, 0, 0, T), pick(b, 1, 0, T)
+
+        fill_window(1, 2)
+        fill_window(2, 3)
+        fill_window(3, 4)
+        summed0 = sum_by_token(0, *both(0), 3)
+        fill_window(4, 4)
+        fill_window(5, 2)
+        turn_back(0, summed0, 7)
+        fill_window(6, 3)
+        summed = sum_by_token(1, *both(1), 4)
+        fill_window(7, 7)
+        for b in range(2, TENSOR_SUMS):
+            ahead = sum_by_token(b, *both(b), 3 + b % 2)
+            turn_back(b - 1, summed, 2 if b % 2 == 0 else 7)
+            summed = ahead
+        turn_back(TENSOR_SUMS - 1, summed, 2 if TENSOR_SUMS % 2 == 0 else 7)
 
         waiting = None
-        for b in range(ROW_BLOCKS - 1):
+        for b in range(TENSOR_SUMS, ROW_BLOCKS - 1):
             first = pick(b, 0, 0, T)
             if waiting is not None:
                 add_on_vector(b - 1, *waiting, 0, T)
             second = pick(b, 1, 0, T)
-            if b < TENSOR_SUMS:
-                add_on_tensor(b, first, second)
-            else:
-                waiting = (first, second)
+            waiting = (first, second)
         last = ROW_BLOCKS - 1
         cut = T - TAIL
         head_first = pick(last, 0, 0, cut)

@@ -22,7 +22,7 @@ ROW_BLOCKS = K // P
 LAST_EXPERT = E - 1
 HALF_H = H // 2
 W2_PIECES = [(0, 2), (2, 5), (5, 8)]
-TENSOR_SUMS = 6
+TENSOR_SUMS = ROW_BLOCKS - 2
 TAIL = 128
 
 
@@ -115,8 +115,9 @@ def tile_moe_cpy_mlp_relu2_kernel(
             nc.sync.dma_start(out=gate_sb[r][:], in_=gate[r])
         load_xr(1)
         load_w2(1)
+        load_xr(2)
         load_w2(2)
-        for b in range(2, ROW_BLOCKS):
+        for b in range(3, ROW_BLOCKS):
             load_xr(b)
 
         for b in range(ROW_BLOCKS):
@@ -262,38 +263,29 @@ def tile_moe_cpy_mlp_relu2_kernel(
 
         nc.scalar.copy(*second_layer(0, list(range(LAST_EXPERT)), 0))
         nc.vector.tensor_copy(*second_layer(0, [LAST_EXPERT], 1))
-
         def fill_window(b, n):
             nc.scalar.copy(*second_layer(b, list(range(E)), n))
 
         def both(b):
             return pick(b, 0, 0, T), pick(b, 1, 0, T)
 
-        fill_window(1, 2)
-        fill_window(2, 3)
-        fill_window(3, 4)
-        summed0 = sum_by_token(0, *both(0), 3)
-        fill_window(4, 4)
-        fill_window(5, 2)
-        turn_back(0, summed0, 7)
-        fill_window(6, 3)
-        summed = sum_by_token(1, *both(1), 4)
-        fill_window(7, 7)
-        for b in range(2, TENSOR_SUMS):
-            ahead = sum_by_token(b, *both(b), 3 + b % 2)
-            turn_back(b - 1, summed, 2 if b % 2 == 0 else 7)
+        for b in range(1, 5):
+            fill_window(b, b + 1)
+        summed = sum_by_token(0, *both(0), 3)
+        fill_window(5, 7)
+        late = [second_layer(b, list(range(E)), n) for b, n in ((6, 6), (7, 0))]
+        for b in range(1, TENSOR_SUMS):
+            ahead = sum_by_token(b, *both(b), 7 if b % 2 else 6)
+            turn_back(b - 1, summed, 1 if b % 2 else 2)
             summed = ahead
-        turn_back(TENSOR_SUMS - 1, summed, 2 if TENSOR_SUMS % 2 == 0 else 7)
+            if b == 1:
+                for copy in late:
+                    nc.scalar.copy(*copy)
+        turn_back(TENSOR_SUMS - 1, summed, 4)
 
-        waiting = None
-        for b in range(TENSOR_SUMS, ROW_BLOCKS - 1):
-            first = pick(b, 0, 0, T)
-            if waiting is not None:
-                add_on_vector(b - 1, *waiting, 0, T)
-            second = pick(b, 1, 0, T)
-            waiting = (first, second)
         last = ROW_BLOCKS - 1
         cut = T - TAIL
+        waiting = both(last - 1)
         head_first = pick(last, 0, 0, cut)
         add_on_vector(last - 1, *waiting, 0, T)
         head_second = pick(last, 1, 0, cut)

@@ -53,8 +53,8 @@ def tile_moe_cpy_mlp_relu2_kernel(
         zeros = keep.tile([P, PAD], F32, name="zeros")
         ident = keep.tile([P, P], F32, name="ident")
 
-        nc.gpsimd.memset(w1s[0][:].bitcast(I32), 0)
-        for scales in (xs, w1s[1], w2s):
+        nc.gpsimd.memset(xs[:].bitcast(I32), 0)
+        for scales in (w1s[0], w1s[1], w2s):
             nc.vector.memset(scales[:].bitcast(I32), 0)
         nc.vector.memset(zeros[:], 0.0)
 
@@ -92,14 +92,13 @@ def tile_moe_cpy_mlp_relu2_kernel(
                 )
 
         nc.sync.dma_start(out=offs_sb[:], in_=offs)
-        load_scales(w1s[0], w1_passes[0:4], range(2))
-        load_scales(xs, x_scales, range(4))
         nc.sync.dma_start(
             out=xw[:].bitcast(I32).rearrange("p (s t) -> p s t", s=2),
             in_=x_words.rearrange("s p t d -> p s (t d)").bitcast(I32),
         )
-        load_scales(w1s[0], w1_passes[0:4], range(2, 4))
+        load_scales(xs, x_scales, range(4))
         load_w1(0)
+        load_scales(w1s[0], w1_passes[0:4], range(4))
         load_w1(1)
         load_scales(w1s[1], w1_passes[4:8], range(4))
         load_w1(2)
@@ -130,7 +129,7 @@ def tile_moe_cpy_mlp_relu2_kernel(
             picks = offs_sb[:, e * C // 16 : (e + 1) * C // 16]
             slot_words[e] = []
             for s in range(2):
-                words = keep.tile([P, C], U32, name=f"slot_words{e}_{s}", align_bytes=64)
+                words = keep.tile([P, C], U32, name=f"slot_words{e}_{s}", tag=f"slot_words{e % 2}_{s}", align_bytes=64)
                 nc.vector.tensor_copy(words[:], xw[:, s * T : (s + 1) * T].indirect(picks))
                 slot_words[e].append(words)
             slot_scales[e] = keep.tile([P, C], U8, name=f"slot_scales{e}", align_bytes=64)
@@ -230,13 +229,15 @@ def tile_moe_cpy_mlp_relu2_kernel(
             nc.vector.tensor_tensor(result[:], first[:], second[:], ALU.add)
             nc.sync.dma_start(out=out[b * P : (b + 1) * P, lo:hi], in_=result[:])
 
-        for e in range(E):
-            gather_slots(e)
+        gather_slots(0)
+        gather_slots(1)
 
         sums0 = first_layer(0, w1w[0], 0, H, 0)
+        gather_slots(2)
         relu0 = relu_tile(0)
         nc.scalar.activation(relu0[:], by_byte(sums0), ACT.Relu)
         sums1 = first_layer(1, w1w[1], 0, H, 1)
+        gather_slots(LAST_EXPERT)
         turn_and_square(0, relu0, 5)
         sums2 = first_layer(2, w1w[2], 0, H, 2)
         pairs1 = square_into_pairs(sums1, "w1w2")

@@ -206,11 +206,11 @@ def tile_moe_cpy_mlp_relu2_kernel(
 
         def sum_by_token(b, first, second, n):
             by_token = bank(n, [P, T // P, P])
-            for c in range(T // P):
-                for r, product in enumerate((first, second)):
+            for r, product in enumerate((first, second)):
+                for c in range(T // P):
                     nc.tensor.matmul(
                         by_token[:, c, :], product[:, c * P : (c + 1) * P], ident[:],
-                        start=(r == 0), stop=(r == 1), is_transpose=True,
+                        start=(r == 0 and c == 0), stop=(r == 1 and c == T // P - 1), is_transpose=True,
                     )
             summed = keep.tile([P, T // P, P], F32, name=f"summed{b}")
             nc.scalar.copy(summed[:], by_token[:])

@@ -43,7 +43,7 @@ def tile_moe_cpy_mlp_relu2_kernel(
         xs = keep.tile([P, T], U8, name="xs", align_bytes=64)
         w1w = [keep.tile([P, 2, H], U32, name=f"w1w{e}", tag=f"w1w{e}", align_bytes=64) for e in range(LAST_EXPERT)]
         w1w_last = [
-            keep.tile([P, 2, HALF_H], U32, name=f"w1w_last{h}", tag=f"w1w_last{h}", align_bytes=64) for h in range(2)
+            keep.tile([P, H], U32, name=f"w1w_last{s}", tag=f"w1w_last{s}", align_bytes=64) for s in range(2)
         ]
         w1s = [keep.tile([P, H], U8, name=f"w1s{j}", align_bytes=64) for j in range(2)]
         w2w = [keep.tile([P, E, (b1 - b0) * P], U32, name=f"w2w{b0}", align_bytes=64) for b0, b1 in W2_PIECES]
@@ -54,7 +54,8 @@ def tile_moe_cpy_mlp_relu2_kernel(
         ident = keep.tile([P, P], F32, name="ident")
 
         nc.gpsimd.memset(xs[:].bitcast(I32), 0)
-        for scales in (w1s[0], w1s[1], w2s):
+        nc.gpsimd.memset(w2s[:].bitcast(I32), 0)
+        for scales in w1s:
             nc.vector.memset(scales[:].bitcast(I32), 0)
         nc.vector.memset(zeros[:], 0.0)
 
@@ -83,30 +84,28 @@ def tile_moe_cpy_mlp_relu2_kernel(
         def load_xr(b):
             nc.sync.dma_start(out=window[b][:, SLOTS : SLOTS + T], in_=xr[b * P : (b + 1) * P, :])
 
-        def load_scales(scales, passes, quadrants):
+        def load_scales(scales, passes, queue):
             count = passes.shape[0]
-            for q in quadrants:
-                nc.sync.dma_start(
+            for q in range(4):
+                queue.dma_start(
                     out=scales[32 * q : 32 * q + 4 * count, :].bitcast(I32),
                     in_=passes[:, 4 * q : 4 * q + 4, :].bitcast(I32),
                 )
 
-        nc.sync.dma_start(out=offs_sb[:], in_=offs)
         nc.sync.dma_start(
             out=xw[:].bitcast(I32).rearrange("p (s t) -> p s t", s=2),
             in_=x_words.rearrange("s p t d -> p s (t d)").bitcast(I32),
         )
-        load_scales(xs, x_scales, range(4))
+        nc.sync.dma_start(out=offs_sb[:], in_=offs)
+        load_scales(xs, x_scales, nc.sync)
         load_w1(0)
-        load_scales(w1s[0], w1_passes[0:4], range(4))
+        load_scales(w1s[0], w1_passes[0:4], nc.sync)
         load_w1(1)
-        load_scales(w1s[1], w1_passes[4:8], range(4))
+        load_scales(w1s[1], w1_passes[4:8], nc.sync)
         load_w1(2)
-        for h in range(2):
-            nc.sync.dma_start(
-                out=w1w_last[h][:].bitcast(I32), in_=w1_src[LAST_EXPERT][:, :, h * HALF_H : (h + 1) * HALF_H]
-            )
-        load_scales(w2s, w2_scales.rearrange("e s b n -> (e s) b n"), range(4))
+        for s in range(2):
+            nc.sync.dma_start(out=w1w_last[s][:].bitcast(I32), in_=w1_src[LAST_EXPERT][:, s, :])
+        load_scales(w2s, w2_scales.rearrange("e s b n -> (e s) b n"), nc.gpsimd)
         load_w2(0)
         load_xr(0)
         for r, pos in enumerate((pos1, pos2)):
@@ -139,19 +138,22 @@ def tile_moe_cpy_mlp_relu2_kernel(
         h_scales = [keep.tile([P, C], U8, name=f"h_scales{e}", align_bytes=64) for e in range(E)]
         h_bf = [keep.tile([P, C, 4], BF16, name=f"h_bf{e}", align_bytes=64) for e in range(E)]
 
-        def first_layer(e, words, lo, hi, n):
-            sums = bank(n, [P, hi - lo])
+        def first_pass(e, s, words, sums, lo, hi):
+            place = 2 * (e % 2) + s
+            nc.tensor.matmul_mx(
+                out=sums[:],
+                lhsT=slot_words[e][s][:].bitcast(FP8X4),
+                lhsT_scale=slot_scales[e][4 * s : P, :],
+                rhs=words[:, lo:hi].bitcast(FP8X4),
+                rhs_scale=w1s[e // 2][4 * place : P, lo:hi],
+                start=(s == 0),
+                stop=(s == 1),
+            )
+
+        def first_layer(e, n):
+            sums = bank(n, [P, H])
             for s in range(2):
-                place = 2 * (e % 2) + s
-                nc.tensor.matmul_mx(
-                    out=sums[:],
-                    lhsT=slot_words[e][s][:].bitcast(FP8X4),
-                    lhsT_scale=slot_scales[e][4 * s : P, :],
-                    rhs=words[:, s, :].bitcast(FP8X4),
-                    rhs_scale=w1s[e // 2][4 * place : P, lo:hi],
-                    start=(s == 0),
-                    stop=(s == 1),
-                )
+                first_pass(e, s, w1w[e][:, s, :], sums, 0, H)
             return sums
 
         def by_byte(sums):
@@ -232,21 +234,24 @@ def tile_moe_cpy_mlp_relu2_kernel(
         gather_slots(0)
         gather_slots(1)
 
-        sums0 = first_layer(0, w1w[0], 0, H, 0)
+        sums0 = first_layer(0, 0)
         gather_slots(2)
         relu0 = relu_tile(0)
         nc.scalar.activation(relu0[:], by_byte(sums0), ACT.Relu)
-        sums1 = first_layer(1, w1w[1], 0, H, 1)
+        sums1 = first_layer(1, 1)
         gather_slots(LAST_EXPERT)
         turn_and_square(0, relu0, 5)
-        sums2 = first_layer(2, w1w[2], 0, H, 2)
+        sums2 = first_layer(2, 2)
         pairs1 = square_into_pairs(sums1, "w1w2")
         relu2 = relu_tile(2)
         nc.vector.tensor_scalar_max(relu2[:], by_byte(sums2), 0.0)
-        sums3a = first_layer(LAST_EXPERT, w1w_last[0], 0, HALF_H, 3)
+        sums3a = bank(3, [P, HALF_H])
+        sums3b = bank(4, [P, HALF_H])
+        for s in range(2):
+            first_pass(LAST_EXPERT, s, w1w_last[s][:], sums3a, 0, HALF_H)
+            first_pass(LAST_EXPERT, s, w1w_last[s][:], sums3b, HALF_H, H)
         relu3 = relu_tile(LAST_EXPERT)
         nc.scalar.activation(relu3[:, :, 0 : P // 2], by_byte(sums3a), ACT.Relu)
-        sums3b = first_layer(LAST_EXPERT, w1w_last[1], HALF_H, H, 4)
         nc.vector.tensor_scalar_max(relu3[:, :, P // 2 : P], by_byte(sums3b), 0.0)
         turn_and_square(2, relu2, 7)
         turn_pairs(1, pairs1, 6)

@@ -54,8 +54,7 @@ def tile_moe_cpy_mlp_relu2_kernel(
         ident = keep.tile([P, P], F32, name="ident")
 
         nc.gpsimd.memset(xs[:].bitcast(I32), 0)
-        nc.gpsimd.memset(w2s[:].bitcast(I32), 0)
-        for scales in w1s:
+        for scales in (w1s[0], w1s[1], w2s):
             nc.vector.memset(scales[:].bitcast(I32), 0)
         nc.vector.memset(zeros[:], 0.0)
 
@@ -73,6 +72,11 @@ def tile_moe_cpy_mlp_relu2_kernel(
         w1_src = w1_words.rearrange("e s p i d -> e p s (i d)").bitcast(I32)
         w2_src = w2_words.rearrange("e s p n d -> p (e s) (n d)").bitcast(I32)
         w1_passes = w1_scales.rearrange("e s b i -> (e s) b i")
+
+        def load_x(s):
+            nc.sync.dma_start(
+                out=xw[:, s * T : (s + 1) * T].bitcast(I32), in_=x_words[s].rearrange("p t d -> p (t d)").bitcast(I32)
+            )
 
         def load_w1(e):
             nc.sync.dma_start(out=w1w[e][:].bitcast(I32), in_=w1_src[e])
@@ -92,20 +96,18 @@ def tile_moe_cpy_mlp_relu2_kernel(
                     in_=passes[:, 4 * q : 4 * q + 4, :].bitcast(I32),
                 )
 
-        nc.sync.dma_start(
-            out=xw[:].bitcast(I32).rearrange("p (s t) -> p s t", s=2),
-            in_=x_words.rearrange("s p t d -> p s (t d)").bitcast(I32),
-        )
+        load_x(0)
         nc.sync.dma_start(out=offs_sb[:], in_=offs)
         load_scales(xs, x_scales, nc.sync)
+        load_x(1)
         load_w1(0)
         load_scales(w1s[0], w1_passes[0:4], nc.sync)
         load_w1(1)
-        load_scales(w1s[1], w1_passes[4:8], nc.sync)
         load_w1(2)
+        load_scales(w1s[1], w1_passes[4:8], nc.sync)
         for s in range(2):
             nc.sync.dma_start(out=w1w_last[s][:].bitcast(I32), in_=w1_src[LAST_EXPERT][:, s, :])
-        load_scales(w2s, w2_scales.rearrange("e s b n -> (e s) b n"), nc.gpsimd)
+        load_scales(w2s, w2_scales.rearrange("e s b n -> (e s) b n"), nc.sync)
         load_w2(0)
         load_xr(0)
         for r, pos in enumerate((pos1, pos2)):
@@ -128,8 +130,9 @@ def tile_moe_cpy_mlp_relu2_kernel(
             picks = offs_sb[:, e * C // 16 : (e + 1) * C // 16]
             slot_words[e] = []
             for s in range(2):
-                words = keep.tile([P, C], U32, name=f"slot_words{e}_{s}", tag=f"slot_words{e % 2}_{s}", align_bytes=64)
-                nc.vector.tensor_copy(words[:], xw[:, s * T : (s + 1) * T].indirect(picks))
+                words = keep.tile([P, C], U32, name=f"slot_words{e}_{s}", align_bytes=64)
+                end = T if e == 0 and s == 0 else 2 * T
+                nc.vector.tensor_copy(words[:], xw[:, s * T : end].indirect(picks))
                 slot_words[e].append(words)
             slot_scales[e] = keep.tile([P, C], U8, name=f"slot_scales{e}", align_bytes=64)
             nc.vector.tensor_copy(slot_scales[e][:], xs[:].indirect(picks))
@@ -168,10 +171,10 @@ def tile_moe_cpy_mlp_relu2_kernel(
                 nc.tensor.transpose(turned[:, d, :], relu[:, d, :], ident[:])
             nc.scalar.activation(h_bf[e][:], turned[:].rearrange("p d c -> p c d"), ACT.Square)
 
-        def square_into_pairs(sums, tag):
+        def square_into_pairs(sums):
             relu = keep.tile([P, 2, P, 2], F32, name="relu_pairs")
-            nc.scalar.activation(relu[:], sums[:].rearrange("p (m u t) -> p u m t", u=2, t=2), ACT.Relu)
-            pairs = keep.tile([P, H], BF16, name="pairs", tag=tag, align_bytes=64)
+            nc.vector.tensor_scalar_max(relu[:], sums[:].rearrange("p (m u t) -> p u m t", u=2, t=2), 0.0)
+            pairs = keep.tile([P, H], BF16, name="pairs", align_bytes=64)
             nc.scalar.activation(pairs[:], relu[:].rearrange("p u m t -> p (u m t)"), ACT.Square)
             return pairs
 
@@ -231,18 +234,16 @@ def tile_moe_cpy_mlp_relu2_kernel(
             nc.vector.tensor_tensor(result[:], first[:], second[:], ALU.add)
             nc.sync.dma_start(out=out[b * P : (b + 1) * P, lo:hi], in_=result[:])
 
-        gather_slots(0)
-        gather_slots(1)
+        for e in range(E):
+            gather_slots(e)
 
         sums0 = first_layer(0, 0)
-        gather_slots(2)
         relu0 = relu_tile(0)
         nc.scalar.activation(relu0[:], by_byte(sums0), ACT.Relu)
         sums1 = first_layer(1, 1)
-        gather_slots(LAST_EXPERT)
         turn_and_square(0, relu0, 5)
         sums2 = first_layer(2, 2)
-        pairs1 = square_into_pairs(sums1, "w1w2")
+        pairs1 = square_into_pairs(sums1)
         relu2 = relu_tile(2)
         nc.vector.tensor_scalar_max(relu2[:], by_byte(sums2), 0.0)
         sums3a = bank(3, [P, HALF_H])
@@ -254,7 +255,7 @@ def tile_moe_cpy_mlp_relu2_kernel(
         nc.scalar.activation(relu3[:, :, 0 : P // 2], by_byte(sums3a), ACT.Relu)
         nc.vector.tensor_scalar_max(relu3[:, :, P // 2 : P], by_byte(sums3b), 0.0)
         turn_and_square(2, relu2, 7)
-        turn_pairs(1, pairs1, 6)
+        turn_pairs(1, pairs1, 2)
         turn_and_square(LAST_EXPERT, relu3, 5)
 
         h_early = keep.tile([P, LAST_EXPERT * C], U32, name="h_early", tag="w1w_last1", align_bytes=64)

@@ -21,7 +21,7 @@ WINDOW = SLOTS + T + PAD
 ROW_BLOCKS = K // P
 LAST_EXPERT = E - 1
 HALF_H = H // 2
-W2_PIECES = [(0, 2), (2, 5), (5, 8)]
+W2_PIECES = [(0, 3), (3, 5), (5, 8)]
 TENSOR_SUMS = ROW_BLOCKS - 2
 TAIL = 128
 
@@ -49,6 +49,7 @@ def tile_moe_cpy_mlp_relu2_kernel(
         w2w = [keep.tile([P, E, (b1 - b0) * P], U32, name=f"w2w{b0}", align_bytes=64) for b0, b1 in W2_PIECES]
         w2s = keep.tile([P, K], U8, name="w2s", align_bytes=64)
         gate_sb = [keep.tile([P, T], F32, name=f"gate_sb{r}") for r in range(2)]
+        gate_t = [keep.tile([P, T // P], F32, name=f"gate_t{r}") for r in range(2)]
         window = [keep.tile([P, WINDOW], F32, name=f"window{b}") for b in range(ROW_BLOCKS)]
         zeros = keep.tile([P, PAD], F32, name="zeros")
         ident = keep.tile([P, P], F32, name="ident")
@@ -110,14 +111,18 @@ def tile_moe_cpy_mlp_relu2_kernel(
         load_scales(w2s, w2_scales.rearrange("e s b n -> (e s) b n"), nc.sync)
         load_w2(0)
         load_xr(0)
-        for r, pos in enumerate((pos1, pos2)):
-            nc.sync.dma_start(out=pos_sb[r][:], in_=pos)
-            nc.sync.dma_start(out=gate_sb[r][:], in_=gate[r])
-        load_xr(1)
-        load_w2(1)
+        nc.sync.dma_start(out=pos_sb[0][:], in_=pos1)
+        nc.sync.dma_start(out=gate_sb[0][:], in_=gate[0])
+        nc.sync.dma_start(out=pos_sb[1][:], in_=pos2)
         load_xr(2)
+        nc.sync.dma_start(out=gate_sb[1][:], in_=gate[1])
+        load_w2(1)
+        load_xr(1)
+        with nc.allow_non_contiguous_dma(reason="one gate value a partition"):
+            for r in range(2):
+                nc.sync.dma_start(out=gate_t[r][:], in_=gate[r, 0, :].rearrange("(c p) -> p c", p=P))
         load_w2(2)
-        for b in range(3, ROW_BLOCKS):
+        for b in (3, 5, 4, 6, 7):
             load_xr(b)
 
         for b in range(ROW_BLOCKS):
@@ -209,25 +214,44 @@ def tile_moe_cpy_mlp_relu2_kernel(
             )
             return product
 
-        def sum_by_token(b, first, second, n):
-            by_token = bank(n, [P, T // P, P])
-            for r, product in enumerate((first, second)):
-                for c in range(T // P):
-                    nc.tensor.matmul(
-                        by_token[:, c, :], product[:, c * P : (c + 1) * P], ident[:],
-                        start=(r == 0 and c == 0), stop=(r == 1 and c == T // P - 1), is_transpose=True,
-                    )
-            summed = keep.tile([P, T // P, P], F32, name=f"summed{b}")
-            nc.scalar.copy(summed[:], by_token[:])
-            return summed
+        def fetch(b, r, lo, hi):
+            fetched = keep.tile([P, hi - lo], F32, name=f"fetched{b}_{r}_{lo}")
+            nc.scalar.activation(fetched[:], window[b][:].indirect(pos_sb[r][:, lo // 16 : hi // 16]), ACT.Copy)
+            return fetched
 
-        def turn_back(b, summed, n):
-            by_row = bank(n, [P, T // P, P])
-            for c in range(T // P):
-                nc.tensor.transpose(by_row[:, c, :], summed[:, c, :], ident[:])
-            result = keep.tile([P, T], F32, name=f"result{b}")
+        def turn(fetched, n):
+            chunks = fetched.shape[1] // P
+            by_token = bank(n, [P, chunks, P])
+            for c in range(chunks):
+                nc.tensor.transpose(by_token[:, c, :], fetched[:, c * P : (c + 1) * P], ident[:])
+            return by_token
+
+        def weigh(b, r, lo, by_token):
+            chunks = by_token.shape[1]
+            product = keep.tile([P, chunks, P], F32, name=f"weighed{b}_{r}_{lo}")
+            for c in range(chunks):
+                column = lo // P + c
+                nc.scalar.activation(
+                    product[:, c, :], by_token[:, c, :], ACT.Copy, scale=gate_t[r][:, column : column + 1]
+                )
+            return product
+
+        def turn_back(first, second, n):
+            chunks = first.shape[1]
+            by_row = bank(n, [P, chunks, P])
+            for r, product in enumerate((first, second)):
+                for c in range(chunks):
+                    nc.tensor.matmul(
+                        by_row[:, c, :], product[:, c, :], ident[:],
+                        start=(r == 0 and c == 0), stop=(r == 1 and c == chunks - 1), is_transpose=True,
+                    )
+            return by_row
+
+        def store_sum(b, lo, by_row):
+            width = by_row.shape[1] * P
+            result = keep.tile([P, width], F32, name=f"result{b}_{lo}")
             nc.scalar.copy(result[:], by_row[:].rearrange("p c t -> p (c t)"))
-            nc.scalar.dma_start(out=out[b * P : (b + 1) * P, :], in_=result[:])
+            nc.sync.dma_start(out=out[b * P : (b + 1) * P, lo : lo + width], in_=result[:])
 
         def add_on_vector(b, first, second, lo, hi):
             result = keep.tile([P, hi - lo], F32, name=f"result{b}_{lo}")
@@ -273,30 +297,36 @@ def tile_moe_cpy_mlp_relu2_kernel(
         def fill_window(b, n):
             nc.scalar.copy(*second_layer(b, list(range(E)), n))
 
-        def both(b):
-            return pick(b, 0, 0, T), pick(b, 1, 0, T)
+        def on_scalar(b, lo, hi, banks):
+            first = fetch(b, 0, lo, hi)
+            second = fetch(b, 1, lo, hi)
+            first = weigh(b, 0, lo, turn(first, banks[0]))
+            second = weigh(b, 1, lo, turn(second, banks[1]))
+            return turn_back(first, second, banks[2])
 
-        for b in range(1, 5):
-            fill_window(b, b + 1)
-        summed = sum_by_token(0, *both(0), 3)
+        def on_vector(b, lo, hi, waiting):
+            first = pick(b, 0, lo, hi)
+            if waiting:
+                add_on_vector(*waiting)
+            return (b, first, pick(b, 1, lo, hi), lo, hi)
+
+        fill_window(1, 2)
+        fill_window(2, 3)
+        waiting = on_vector(0, 0, T, None)
+        fill_window(3, 4)
+        fill_window(4, 6)
         fill_window(5, 7)
-        late = [second_layer(b, list(range(E)), n) for b, n in ((6, 6), (7, 0))]
-        for b in range(1, TENSOR_SUMS):
-            ahead = sum_by_token(b, *both(b), 7 if b % 2 else 6)
-            turn_back(b - 1, summed, 1 if b % 2 else 2)
-            summed = ahead
-            if b == 1:
-                for copy in late:
-                    nc.scalar.copy(*copy)
-        turn_back(TENSOR_SUMS - 1, summed, 4)
-
-        last = ROW_BLOCKS - 1
-        cut = T - TAIL
-        waiting = both(last - 1)
-        head_first = pick(last, 0, 0, cut)
-        add_on_vector(last - 1, *waiting, 0, T)
-        head_second = pick(last, 1, 0, cut)
-        tail_first = pick(last, 0, cut, T)
-        add_on_vector(last, head_first, head_second, 0, cut)
-        tail_second = pick(last, 1, cut, T)
-        add_on_vector(last, tail_first, tail_second, cut, T)
+        sum2 = on_scalar(2, 0, T, (4, 6, 7))
+        waiting = on_vector(1, 0, T, waiting)
+        fill_window(6, 0)
+        fill_window(7, 1)
+        waiting = on_vector(3, 0, T, waiting)
+        store_sum(2, 0, sum2)
+        sum5 = on_scalar(5, 0, T, (0, 1, 2))
+        waiting = on_vector(4, 0, T, waiting)
+        store_sum(5, 0, sum5)
+        waiting = on_vector(6, 0, T, waiting)
+        sum7 = on_scalar(7, T // 2, T, (3, 4, 5))
+        waiting = on_vector(7, 0, T // 2, waiting)
+        add_on_vector(*waiting)
+        store_sum(7, T // 2, sum7)

@@ -21,7 +21,7 @@ WINDOW = SLOTS + T + PAD
 ROW_BLOCKS = K // P
 LAST_EXPERT = E - 1
 HALF_H = H // 2
-W2_PIECES = [(0, 3), (3, 5), (5, 8)]
+W2_PIECES = [(0, 2), (2, 5), (5, 8)]
 TENSOR_SUMS = ROW_BLOCKS - 2
 TAIL = 128
 
@@ -49,12 +49,14 @@ def tile_moe_cpy_mlp_relu2_kernel(
         w2w = [keep.tile([P, E, (b1 - b0) * P], U32, name=f"w2w{b0}", align_bytes=64) for b0, b1 in W2_PIECES]
         w2s = keep.tile([P, K], U8, name="w2s", align_bytes=64)
         gate_sb = [keep.tile([P, T], F32, name=f"gate_sb{r}") for r in range(2)]
-        gate_t = [keep.tile([P, T // P], F32, name=f"gate_t{r}") for r in range(2)]
+        gate_rows = keep.tile([P, P], F32, name="gate_rows")
+        gate_t = keep.tile([P, 2 * T // P], F32, name="gate_t")
         window = [keep.tile([P, WINDOW], F32, name=f"window{b}") for b in range(ROW_BLOCKS)]
         zeros = keep.tile([P, PAD], F32, name="zeros")
         ident = keep.tile([P, P], F32, name="ident")
 
         nc.gpsimd.memset(xs[:].bitcast(I32), 0)
+        nc.gpsimd.memset(gate_rows[:], 0.0)
         for scales in (w1s[0], w1s[1], w2s):
             nc.vector.memset(scales[:].bitcast(I32), 0)
         nc.vector.memset(zeros[:], 0.0)
@@ -108,22 +110,22 @@ def tile_moe_cpy_mlp_relu2_kernel(
         load_scales(w1s[1], w1_passes[4:8], nc.sync)
         for s in range(2):
             nc.sync.dma_start(out=w1w_last[s][:].bitcast(I32), in_=w1_src[LAST_EXPERT][:, s, :])
-        load_scales(w2s, w2_scales.rearrange("e s b n -> (e s) b n"), nc.sync)
         load_w2(0)
-        load_xr(0)
         nc.sync.dma_start(out=pos_sb[0][:], in_=pos1)
-        nc.sync.dma_start(out=gate_sb[0][:], in_=gate[0])
         nc.sync.dma_start(out=pos_sb[1][:], in_=pos2)
-        load_xr(2)
+        load_xr(0)
+        nc.sync.dma_start(out=gate_sb[0][:], in_=gate[0])
+        nc.sync.dma_start(out=gate_rows[0 : 2 * T // P, :], in_=gate[:, 0, :].rearrange("r (c t) -> r c t", t=P))
+        load_xr(1)
         nc.sync.dma_start(out=gate_sb[1][:], in_=gate[1])
         load_w2(1)
-        load_xr(1)
-        with nc.allow_non_contiguous_dma(reason="one gate value a partition"):
-            for r in range(2):
-                nc.sync.dma_start(out=gate_t[r][:], in_=gate[r, 0, :].rearrange("(c p) -> p c", p=P))
+        load_xr(2)
+        load_xr(3)
         load_w2(2)
-        for b in (3, 5, 4, 6, 7):
+        for b in (4, 6, 5, 7):
             load_xr(b)
+
+        load_scales(w2s, w2_scales.rearrange("e s b n -> (e s) b n"), nc.gpsimd)
 
         for b in range(ROW_BLOCKS):
             nc.scalar.activation(window[b][:, SLOTS + T : WINDOW], zeros[:], ACT.Square)
@@ -215,7 +217,7 @@ def tile_moe_cpy_mlp_relu2_kernel(
             return product
 
         def fetch(b, r, lo, hi):
-            fetched = keep.tile([P, hi - lo], F32, name=f"fetched{b}_{r}_{lo}")
+            fetched = keep.tile([P, hi - lo], F32, name=f"fetched{b}_{r}_{lo}", tag=f"fetched{b}_{r}")
             nc.scalar.activation(fetched[:], window[b][:].indirect(pos_sb[r][:, lo // 16 : hi // 16]), ACT.Copy)
             return fetched
 
@@ -230,9 +232,9 @@ def tile_moe_cpy_mlp_relu2_kernel(
             chunks = by_token.shape[1]
             product = keep.tile([P, chunks, P], F32, name=f"weighed{b}_{r}_{lo}")
             for c in range(chunks):
-                column = lo // P + c
+                column = r * T // P + lo // P + c
                 nc.scalar.activation(
-                    product[:, c, :], by_token[:, c, :], ACT.Copy, scale=gate_t[r][:, column : column + 1]
+                    product[:, c, :], by_token[:, c, :], ACT.Copy, scale=gate_t[:, column : column + 1]
                 )
             return product
 
@@ -247,15 +249,15 @@ def tile_moe_cpy_mlp_relu2_kernel(
                     )
             return by_row
 
-        def store_sum(b, lo, by_row):
+        def store_sum(b, lo, by_row, tag):
             width = by_row.shape[1] * P
-            result = keep.tile([P, width], F32, name=f"result{b}_{lo}")
+            result = keep.tile([P, width], F32, name=f"result{b}_{lo}", tag=tag)
             nc.scalar.copy(result[:], by_row[:].rearrange("p c t -> p (c t)"))
-            nc.sync.dma_start(out=out[b * P : (b + 1) * P, lo : lo + width], in_=result[:])
+            nc.scalar.dma_start(out=out[b * P : (b + 1) * P, lo : lo + width], in_=result[:])
 
         def add_on_vector(b, first, second, lo, hi):
             result = keep.tile([P, hi - lo], F32, name=f"result{b}_{lo}")
-            nc.vector.tensor_tensor(result[:], first[:], second[:], ALU.add)
+            nc.vector.tensor_tensor(result[:], first, second, ALU.add)
             nc.sync.dma_start(out=out[b * P : (b + 1) * P, lo:hi], in_=result[:])
 
         for e in range(E):
@@ -293,7 +295,13 @@ def tile_moe_cpy_mlp_relu2_kernel(
             )
 
         nc.scalar.copy(*second_layer(0, list(range(LAST_EXPERT)), 0))
+        nc.scalar.copy(*second_layer(1, list(range(LAST_EXPERT)), 2))
         nc.vector.tensor_copy(*second_layer(0, [LAST_EXPERT], 1))
+        nc.scalar.copy(*second_layer(1, [LAST_EXPERT], 4))
+        gate_turned = bank(4, [P, P])
+        nc.tensor.transpose(gate_turned[:], gate_rows[:], ident[:])
+        nc.scalar.copy(gate_t[:], gate_turned[:, 0 : 2 * T // P])
+
         def fill_window(b, n):
             nc.scalar.copy(*second_layer(b, list(range(E)), n))
 
@@ -308,25 +316,33 @@ def tile_moe_cpy_mlp_relu2_kernel(
             first = pick(b, 0, lo, hi)
             if waiting:
                 add_on_vector(*waiting)
-            return (b, first, pick(b, 1, lo, hi), lo, hi)
+            return (b, first[:], pick(b, 1, lo, hi)[:], lo, hi)
 
-        fill_window(1, 2)
+        half = T // 2
+        waiting = on_vector(0, 0, half, None)
         fill_window(2, 3)
-        waiting = on_vector(0, 0, T, None)
-        fill_window(3, 4)
-        fill_window(4, 6)
-        fill_window(5, 7)
-        sum2 = on_scalar(2, 0, T, (4, 6, 7))
+        fill_window(3, 0)
+        fill_window(4, 1)
+        sum0 = on_scalar(0, half, T, (3, 0, 7))
         waiting = on_vector(1, 0, T, waiting)
-        fill_window(6, 0)
-        fill_window(7, 1)
-        waiting = on_vector(3, 0, T, waiting)
-        store_sum(2, 0, sum2)
-        sum5 = on_scalar(5, 0, T, (0, 1, 2))
+        waiting = on_vector(2, 0, T, waiting)
+        fill_window(5, 2)
+        fill_window(6, 4)
+        fill_window(7, 6)
+        sum3 = on_scalar(3, 0, T, (2, 4, 5))
+        store_sum(0, half, sum0, "fetched3_0")
         waiting = on_vector(4, 0, T, waiting)
-        store_sum(5, 0, sum5)
-        waiting = on_vector(6, 0, T, waiting)
-        sum7 = on_scalar(7, T // 2, T, (3, 4, 5))
-        waiting = on_vector(7, 0, T // 2, waiting)
+        first = fetch(6, 0, 0, T)
+        second = fetch(6, 1, 0, T)
+        by_token = turn(first, 1)
+        store_sum(3, 0, sum3, "fetched6_0")
+        first = weigh(6, 0, 0, by_token)
+        second = weigh(6, 1, 0, turn(second, 3))
+        waiting = on_vector(5, 0, T, waiting)
+        whole = pick(7, 0, 0, T)
         add_on_vector(*waiting)
-        store_sum(7, T // 2, sum7)
+        ends = [pick(7, 1, lo, lo + half) for lo in (0, half)]
+        for i, lo in enumerate((0, half)):
+            by_row = turn_back(first[:, 2 * i : 2 * i + 2, :], second[:, 2 * i : 2 * i + 2, :], (0, 7)[i])
+            store_sum(6, lo, by_row, f"end{i}")
+            add_on_vector(7, whole[:, lo : lo + half], ends[i][:], lo, lo + half)

@@ -119,10 +119,10 @@ def tile_moe_cpy_mlp_relu2_kernel(
         load_xr(1)
         nc.sync.dma_start(out=gate_sb[1][:], in_=gate[1])
         load_w2(1)
-        load_xr(2)
-        load_xr(3)
+        for b in (2, 3, 4):
+            load_xr(b)
         load_w2(2)
-        for b in (4, 6, 5, 7):
+        for b in (5, 6, 7):
             load_xr(b)
 
         load_scales(w2s, w2_scales.rearrange("e s b n -> (e s) b n"), nc.gpsimd)
@@ -230,7 +230,7 @@ def tile_moe_cpy_mlp_relu2_kernel(
 
         def weigh(b, r, lo, by_token):
             chunks = by_token.shape[1]
-            product = keep.tile([P, chunks, P], F32, name=f"weighed{b}_{r}_{lo}")
+            product = keep.tile([P, chunks, P], F32, name=f"weighed{b}_{r}_{lo}", tag=f"weighed{b}_{r}")
             for c in range(chunks):
                 column = r * T // P + lo // P + c
                 nc.scalar.activation(
@@ -249,14 +249,14 @@ def tile_moe_cpy_mlp_relu2_kernel(
                     )
             return by_row
 
-        def store_sum(b, lo, by_row, tag):
+        def store_sum(b, lo, by_row, tag, queue):
             width = by_row.shape[1] * P
             result = keep.tile([P, width], F32, name=f"result{b}_{lo}", tag=tag)
             nc.scalar.copy(result[:], by_row[:].rearrange("p c t -> p (c t)"))
-            nc.scalar.dma_start(out=out[b * P : (b + 1) * P, lo : lo + width], in_=result[:])
+            queue.dma_start(out=out[b * P : (b + 1) * P, lo : lo + width], in_=result[:])
 
-        def add_on_vector(b, first, second, lo, hi):
-            result = keep.tile([P, hi - lo], F32, name=f"result{b}_{lo}")
+        def add_on_vector(b, first, second, lo, hi, tag):
+            result = keep.tile([P, hi - lo], F32, name=f"result{b}_{lo}", tag=tag)
             nc.vector.tensor_tensor(result[:], first, second, ALU.add)
             nc.sync.dma_start(out=out[b * P : (b + 1) * P, lo:hi], in_=result[:])
 
@@ -312,37 +312,40 @@ def tile_moe_cpy_mlp_relu2_kernel(
             second = weigh(b, 1, lo, turn(second, banks[1]))
             return turn_back(first, second, banks[2])
 
-        def on_vector(b, lo, hi, waiting):
+        def on_vector(b, lo, hi, waiting, tag):
             first = pick(b, 0, lo, hi)
             if waiting:
                 add_on_vector(*waiting)
-            return (b, first[:], pick(b, 1, lo, hi)[:], lo, hi)
+            return (b, first[:], pick(b, 1, lo, hi)[:], lo, hi, tag)
 
         half = T // 2
-        waiting = on_vector(0, 0, half, None)
+        small, whole = pick(0, 0, 0, half), pick(1, 0, 0, T)
+        waiting = (0, small[:], pick(0, 1, 0, half)[:], 0, half, "sum0")
         fill_window(2, 3)
         fill_window(3, 0)
         fill_window(4, 1)
         sum0 = on_scalar(0, half, T, (3, 0, 7))
-        waiting = on_vector(1, 0, T, waiting)
-        waiting = on_vector(2, 0, T, waiting)
+        other = pick(1, 1, 0, T)
+        add_on_vector(*waiting)
+        waiting = (1, whole[:], other[:], 0, T, "fetched0_0")
+        waiting = on_vector(2, 0, T, waiting, "fetched0_1")
         fill_window(5, 2)
         fill_window(6, 4)
         fill_window(7, 6)
         sum3 = on_scalar(3, 0, T, (2, 4, 5))
-        store_sum(0, half, sum0, "fetched3_0")
-        waiting = on_vector(4, 0, T, waiting)
+        store_sum(0, half, sum0, "fetched3_0", nc.gpsimd)
+        waiting = on_vector(4, 0, T, waiting, "fetched3_1")
         first = fetch(6, 0, 0, T)
         second = fetch(6, 1, 0, T)
         by_token = turn(first, 1)
-        store_sum(3, 0, sum3, "fetched6_0")
+        store_sum(3, 0, sum3, "fetched6_0", nc.gpsimd)
         first = weigh(6, 0, 0, by_token)
         second = weigh(6, 1, 0, turn(second, 3))
-        waiting = on_vector(5, 0, T, waiting)
+        waiting = on_vector(5, 0, T, waiting, "weighed3_0")
         whole = pick(7, 0, 0, T)
         add_on_vector(*waiting)
         ends = [pick(7, 1, lo, lo + half) for lo in (0, half)]
         for i, lo in enumerate((0, half)):
             by_row = turn_back(first[:, 2 * i : 2 * i + 2, :], second[:, 2 * i : 2 * i + 2, :], (0, 7)[i])
-            store_sum(6, lo, by_row, f"end{i}")
-            add_on_vector(7, whole[:, lo : lo + half], ends[i][:], lo, lo + half)
+            store_sum(6, lo, by_row, f"end{i}", nc.scalar)
+            add_on_vector(7, whole[:, lo : lo + half], ends[i][:], lo, lo + half, f"last{i}")

@@ -319,12 +319,12 @@ def tile_moe_cpy_mlp_relu2_kernel(
             return (b, first[:], pick(b, 1, lo, hi)[:], lo, hi, tag)
 
         half = T // 2
-        small, whole = pick(0, 0, 0, half), pick(1, 0, 0, T)
-        waiting = (0, small[:], pick(0, 1, 0, half)[:], 0, half, "sum0")
+        small, whole = pick(0, 0, 0, P), pick(1, 0, 0, T)
+        waiting = (0, small[:], pick(0, 1, 0, P)[:], 0, P, "sum0")
         fill_window(2, 3)
         fill_window(3, 0)
         fill_window(4, 1)
-        sum0 = on_scalar(0, half, T, (3, 0, 7))
+        sum0 = on_scalar(0, P, T, (3, 0, 7))
         other = pick(1, 1, 0, T)
         add_on_vector(*waiting)
         waiting = (1, whole[:], other[:], 0, T, "fetched0_0")
@@ -333,7 +333,7 @@ def tile_moe_cpy_mlp_relu2_kernel(
         fill_window(6, 4)
         fill_window(7, 6)
         sum3 = on_scalar(3, 0, T, (2, 4, 5))
-        store_sum(0, half, sum0, "fetched3_0", nc.gpsimd)
+        store_sum(0, P, sum0, "fetched3_0", nc.gpsimd)
         waiting = on_vector(4, 0, T, waiting, "fetched3_1")
         first = fetch(6, 0, 0, T)
         second = fetch(6, 1, 0, T)

@@ -228,9 +228,10 @@ def tile_moe_cpy_mlp_relu2_kernel(
                 nc.tensor.transpose(by_token[:, c, :], fetched[:, c * P : (c + 1) * P], ident[:])
             return by_token
 
-        def weigh(b, r, lo, by_token):
+        def weigh(b, r, lo, by_token, tag=None, product=None):
             chunks = by_token.shape[1]
-            product = keep.tile([P, chunks, P], F32, name=f"weighed{b}_{r}_{lo}", tag=f"weighed{b}_{r}")
+            if product is None:
+                product = keep.tile([P, chunks, P], F32, name=f"weighed{b}_{r}_{lo}", tag=tag or f"weighed{b}_{r}")
             for c in range(chunks):
                 column = r * T // P + lo // P + c
                 nc.scalar.activation(
@@ -305,13 +306,6 @@ def tile_moe_cpy_mlp_relu2_kernel(
         def fill_window(b, n):
             nc.scalar.copy(*second_layer(b, list(range(E)), n))
 
-        def on_scalar(b, lo, hi, banks):
-            first = fetch(b, 0, lo, hi)
-            second = fetch(b, 1, lo, hi)
-            first = weigh(b, 0, lo, turn(first, banks[0]))
-            second = weigh(b, 1, lo, turn(second, banks[1]))
-            return turn_back(first, second, banks[2])
-
         def on_vector(b, lo, hi, waiting, tag):
             first = pick(b, 0, lo, hi)
             if waiting:
@@ -324,28 +318,41 @@ def tile_moe_cpy_mlp_relu2_kernel(
         fill_window(2, 3)
         fill_window(3, 0)
         fill_window(4, 1)
-        sum0 = on_scalar(0, P, T, (3, 0, 7))
+        fetched0 = [fetch(0, r, P, T) for r in range(2)]
+        turned0 = [turn(fetched0[0], 3), turn(fetched0[1], 0)]
+        fetched3 = [fetch(3, r, 0, T) for r in range(2)]
+        turned3 = turn(fetched3[0], 5)
+        both = keep.tile([P, 6, P], F32, name="weighed0", tag="fetched3_0")
+        first = weigh(0, 0, P, turned0[0], product=both[:, 0:3, :])
+        second = weigh(0, 1, P, turned0[1], product=both[:, 3:6, :])
+        first3 = weigh(3, 0, 0, turned3)
         other = pick(1, 1, 0, T)
         add_on_vector(*waiting)
         waiting = (1, whole[:], other[:], 0, T, "fetched0_0")
         waiting = on_vector(2, 0, T, waiting, "fetched0_1")
         fill_window(5, 2)
         fill_window(6, 4)
+        sum0 = turn_back(first, second, 2)
         fill_window(7, 6)
-        sum3 = on_scalar(3, 0, T, (2, 4, 5))
-        store_sum(0, P, sum0, "fetched3_0", nc.gpsimd)
+        by_token = turn(fetched3[1], 4)
+        store_sum(0, P, sum0, "result0", nc.sync)
+        second = weigh(3, 1, 0, by_token)
+        sum3 = turn_back(second, first3, 5)
         waiting = on_vector(4, 0, T, waiting, "fetched3_1")
         first = fetch(6, 0, 0, T)
         second = fetch(6, 1, 0, T)
         by_token = turn(first, 1)
         store_sum(3, 0, sum3, "fetched6_0", nc.gpsimd)
-        first = weigh(6, 0, 0, by_token)
-        second = weigh(6, 1, 0, turn(second, 3))
+        late = [turn(second[:, lo : lo + half], n) for lo, n in ((0, 3), (half, 2))]
+        halves = []
+        for i, lo in enumerate((0, half)):
+            first = weigh(6, 0, lo, by_token[:, 2 * i : 2 * i + 2, :], f"weighed6_0_{i}")
+            halves.append((first, weigh(6, 1, lo, late[i], f"weighed6_1_{i}")))
         waiting = on_vector(5, 0, T, waiting, "weighed3_0")
         whole = pick(7, 0, 0, T)
         add_on_vector(*waiting)
         ends = [pick(7, 1, lo, lo + half) for lo in (0, half)]
         for i, lo in enumerate((0, half)):
-            by_row = turn_back(first[:, 2 * i : 2 * i + 2, :], second[:, 2 * i : 2 * i + 2, :], (0, 7)[i])
+            by_row = turn_back(*halves[i], (0, 7)[i])
             store_sum(6, lo, by_row, f"end{i}", nc.scalar)
             add_on_vector(7, whole[:, lo : lo + half], ends[i][:], lo, lo + half, f"last{i}")

@@ -256,10 +256,13 @@ def tile_moe_cpy_mlp_relu2_kernel(
             nc.scalar.copy(result[:], by_row[:].rearrange("p c t -> p (c t)"))
             queue.dma_start(out=out[b * P : (b + 1) * P, lo : lo + width], in_=result[:])
 
+        def add_into(result, b, first, second, lo, hi):
+            nc.vector.tensor_tensor(result, first, second, ALU.add)
+            nc.sync.dma_start(out=out[b * P : (b + 1) * P, lo:hi], in_=result)
+
         def add_on_vector(b, first, second, lo, hi, tag):
             result = keep.tile([P, hi - lo], F32, name=f"result{b}_{lo}", tag=tag)
-            nc.vector.tensor_tensor(result[:], first, second, ALU.add)
-            nc.sync.dma_start(out=out[b * P : (b + 1) * P, lo:hi], in_=result[:])
+            add_into(result[:], b, first, second, lo, hi)
 
         for e in range(E):
             gather_slots(e)
@@ -338,21 +341,22 @@ def tile_moe_cpy_mlp_relu2_kernel(
         store_sum(0, P, sum0, "result0", nc.sync)
         second = weigh(3, 1, 0, by_token)
         sum3 = turn_back(second, first3, 5)
-        waiting = on_vector(4, 0, T, waiting, "fetched3_1")
+        waiting = on_vector(4, 0, T, waiting, "fetched3_0")
         first = fetch(6, 0, 0, T)
         second = fetch(6, 1, 0, T)
         by_token = turn(first, 1)
-        store_sum(3, 0, sum3, "fetched6_0", nc.gpsimd)
+        store_sum(3, 0, sum3, "fetched6_0", nc.sync)
         late = [turn(second[:, lo : lo + half], n) for lo, n in ((0, 3), (half, 2))]
         halves = []
         for i, lo in enumerate((0, half)):
             first = weigh(6, 0, lo, by_token[:, 2 * i : 2 * i + 2, :], f"weighed6_0_{i}")
             halves.append((first, weigh(6, 1, lo, late[i], f"weighed6_1_{i}")))
-        waiting = on_vector(5, 0, T, waiting, "weighed3_0")
+        waiting = on_vector(5, 0, T, waiting, "fetched3_1")
         whole = pick(7, 0, 0, T)
         add_on_vector(*waiting)
         ends = [pick(7, 1, lo, lo + half) for lo in (0, half)]
+        result7 = keep.tile([P, T], F32, name="result7", tag="fetched6_1")
         for i, lo in enumerate((0, half)):
             by_row = turn_back(*halves[i], (0, 7)[i])
             store_sum(6, lo, by_row, f"end{i}", nc.scalar)
-            add_on_vector(7, whole[:, lo : lo + half], ends[i][:], lo, lo + half, f"last{i}")
+            add_into(result7[:, lo : lo + half], 7, whole[:, lo : lo + half], ends[i][:], lo, lo + half)

from contextlib import ExitStack

import concourse.mybir as mybir

K, T, E, C, H, PAD = 1024, 512, 4, 128, 512, 64
FLOPS = 2 * 2 * K * H * E * C

F32 = mybir.dt.float32
BF16 = mybir.dt.bfloat16
I32 = mybir.dt.int32
U32 = mybir.dt.uint32
U16 = mybir.dt.uint16
U8 = mybir.dt.uint8
FP8X4 = mybir.dt.float8_e4m3fn_x4
ACT = mybir.ActivationFunctionType
ALU = mybir.AluOpType

P = 128
SLOTS = E * C
WINDOW = SLOTS + T + PAD
ROW_BLOCKS = K // P
LAST_EXPERT = E - 1
HALF_H = H // 2
W2_PIECES = [(0, 2), (2, 5), (5, 8)]
TENSOR_SUMS = ROW_BLOCKS - 2
TAIL = 128


def tile_moe_cpy_mlp_relu2_kernel(
    tc, x_words, x_scales, xr, w1_words, w1_scales, w2_words, w2_scales, gate, offs, pos1, pos2, out
):
    nc = tc.nc
    with ExitStack() as ctx:
        keep = ctx.enter_context(tc.tile_pool(name="keep", bufs=1))
        psum = ctx.enter_context(tc.psum_pool(name="psum", bufs=1))

        def bank(n, shape):
            return psum.tile(shape, F32, name=f"bank{n}", tag=f"bank{n}")

        offs_sb = keep.tile([P, SLOTS // 16], U16, name="offs_sb")
        pos_sb = [keep.tile([P, T // 16], U16, name=f"pos_sb{r}") for r in range(2)]
        xw = keep.tile([P, 2 * T], U32, name="xw", align_bytes=64)
        xs = keep.tile([P, T], U8, name="xs", align_bytes=64)
        w1w = [keep.tile([P, 2, H], U32, name=f"w1w{e}", tag=f"w1w{e}", align_bytes=64) for e in range(LAST_EXPERT)]
        w1w_last = [
            keep.tile([P, H], U32, name=f"w1w_last{s}", tag=f"w1w_last{s}", align_bytes=64) for s in range(2)
        ]
        w1s = [keep.tile([P, H], U8, name=f"w1s{j}", align_bytes=64) for j in range(2)]
        w2w = [keep.tile([P, E, (b1 - b0) * P], U32, name=f"w2w{b0}", align_bytes=64) for b0, b1 in W2_PIECES]
        w2s = keep.tile([P, K], U8, name="w2s", align_bytes=64)
        gate_sb = [keep.tile([P, T], F32, name=f"gate_sb{r}") for r in range(2)]
        gate_rows = keep.tile([P, P], F32, name="gate_rows")
        gate_t = keep.tile([P, 2 * T // P], F32, name="gate_t")
        window = [keep.tile([P, WINDOW], F32, name=f"window{b}") for b in range(ROW_BLOCKS)]
        zeros = keep.tile([P, PAD], F32, name="zeros")
        ident = keep.tile([P, P], F32, name="ident")

        nc.gpsimd.memset(xs[:].bitcast(I32), 0)
        nc.gpsimd.memset(gate_rows[:], 0.0)
        for scales in (w1s[0], w1s[1], w2s):
            nc.vector.memset(scales[:].bitcast(I32), 0)
        nc.vector.memset(zeros[:], 0.0)

        ones = keep.tile([P, 32], F32, name="ones")
        column = keep.tile([P, 32], F32, name="column", align_bytes=64)
        row = keep.tile([P, 32], F32, name="row", align_bytes=64)
        nc.vector.memset(ones[:], 1.0)
        nc.vector.memset(ident[:], 0.0)
        nc.vector.tensor_tensor_scan(column[:], ones[:], ones[:], 0.0, ALU.mult, ALU.add)
        nc.vector.transpose(row[:], column[:])
        for q in range(4):
            quad = slice(32 * q, 32 * q + 32)
            nc.vector.tensor_tensor(ident[quad, quad], column[quad, :], row[quad, :], ALU.is_equal)

        w1_src = w1_words.rearrange("e s p i d -> e p s (i d)").bitcast(I32)
        w2_src = w2_words.rearrange("e s p n d -> p (e s) (n d)").bitcast(I32)
        w1_passes = w1_scales.rearrange("e s b i -> (e s) b i")

        def load_x(s):
            nc.sync.dma_start(
                out=xw[:, s * T : (s + 1) * T].bitcast(I32), in_=x_words[s].rearrange("p t d -> p (t d)").bitcast(I32)
            )

        def load_w1(e):
            nc.sync.dma_start(out=w1w[e][:].bitcast(I32), in_=w1_src[e])

        def load_w2(piece):
            b0, b1 = W2_PIECES[piece]
            nc.sync.dma_start(out=w2w[piece][:].bitcast(I32), in_=w2_src[:, :, b0 * P : b1 * P])

        def load_xr(b):
            nc.sync.dma_start(out=window[b][:, SLOTS : SLOTS + T], in_=xr[b * P : (b + 1) * P, :])

        def load_scales(scales, passes, queue):
            count = passes.shape[0]
            for q in range(4):
                queue.dma_start(
                    out=scales[32 * q : 32 * q + 4 * count, :].bitcast(I32),
                    in_=passes[:, 4 * q : 4 * q + 4, :].bitcast(I32),
                )

        load_x(0)
        nc.sync.dma_start(out=offs_sb[:], in_=offs)
        load_scales(xs, x_scales, nc.sync)
        load_x(1)
        load_w1(0)
        load_scales(w1s[0], w1_passes[0:4], nc.sync)
        load_w1(1)
        load_w1(2)
        load_scales(w1s[1], w1_passes[4:8], nc.sync)
        for s in range(2):
            nc.sync.dma_start(out=w1w_last[s][:].bitcast(I32), in_=w1_src[LAST_EXPERT][:, s, :])
        load_w2(0)
        nc.sync.dma_start(out=pos_sb[0][:], in_=pos1)
        nc.sync.dma_start(out=pos_sb[1][:], in_=pos2)
        load_xr(0)
        nc.sync.dma_start(out=gate_sb[0][:], in_=gate[0])
        nc.sync.dma_start(out=gate_rows[0 : 2 * T // P, :], in_=gate[:, 0, :].rearrange("r (c t) -> r c t", t=P))
        load_xr(1)
        nc.sync.dma_start(out=gate_sb[1][:], in_=gate[1])
        load_w2(1)
        for b in (2, 3, 4):
            load_xr(b)
        load_w2(2)
        for b in (5, 6, 7):
            load_xr(b)

        load_scales(w2s, w2_scales.rearrange("e s b n -> (e s) b n"), nc.gpsimd)

        for b in range(ROW_BLOCKS):
            nc.scalar.activation(window[b][:, SLOTS + T : WINDOW], zeros[:], ACT.Square)

        slot_words = {}
        slot_scales = {}

        def gather_slots(e):
            picks = offs_sb[:, e * C // 16 : (e + 1) * C // 16]
            slot_words[e] = []
            for s in range(2):
                words = keep.tile([P, C], U32, name=f"slot_words{e}_{s}", align_bytes=64)
                end = T if e == 0 and s == 0 else 2 * T
                nc.vector.tensor_copy(words[:], xw[:, s * T : end].indirect(picks))
                slot_words[e].append(words)
            slot_scales[e] = keep.tile([P, C], U8, name=f"slot_scales{e}", align_bytes=64)
            nc.vector.tensor_copy(slot_scales[e][:], xs[:].indirect(picks))

        h_words = {}
        h_scales = [keep.tile([P, C], U8, name=f"h_scales{e}", align_bytes=64) for e in range(E)]
        h_bf = [keep.tile([P, C, 4], BF16, name=f"h_bf{e}", align_bytes=64) for e in range(E)]

        def first_pass(e, s, words, sums, lo, hi):
            place = 2 * (e % 2) + s
            nc.tensor.matmul_mx(
                out=sums[:],
                lhsT=slot_words[e][s][:].bitcast(FP8X4),
                lhsT_scale=slot_scales[e][4 * s : P, :],
                rhs=words[:, lo:hi].bitcast(FP8X4),
                rhs_scale=w1s[e // 2][4 * place : P, lo:hi],
                start=(s == 0),
                stop=(s == 1),
            )

        def first_layer(e, n):
            sums = bank(n, [P, H])
            for s in range(2):
                first_pass(e, s, w1w[e][:, s, :], sums, 0, H)
            return sums

        def by_byte(sums):
            return sums[:].rearrange("p (m d) -> p d m", d=4)

        def relu_tile(e):
            return keep.tile([P, 4, P], F32, name=f"relu{e}", align_bytes=64)

        def turn_and_square(e, relu, n):
            turned = bank(n, [P, 4, C])
            for d in range(4):
                nc.tensor.transpose(turned[:, d, :], relu[:, d, :], ident[:])
            nc.scalar.activation(h_bf[e][:], turned[:].rearrange("p d c -> p c d"), ACT.Square)

        def square_into_pairs(sums):
            relu = keep.tile([P, 2, P, 2], F32, name="relu_pairs")
            nc.vector.tensor_scalar_max(relu[:], sums[:].rearrange("p (m u t) -> p u m t", u=2, t=2), 0.0)
            pairs = keep.tile([P, H], BF16, name="pairs", align_bytes=64)
            nc.scalar.activation(pairs[:], relu[:].rearrange("p u m t -> p (u m t)"), ACT.Square)
            return pairs

        def turn_pairs(e, pairs, n):
            turned = bank(n, [P, 2, C])
            as_f32 = pairs[:].bitcast(F32)
            for u in range(2):
                nc.tensor.transpose(turned[:, u, :], as_f32[:, u * P : (u + 1) * P], ident[:])
            dst = h_bf[e][:].rearrange("p c d -> p (c d)").bitcast(F32).rearrange("p (c u) -> p c u", u=2)
            nc.vector.tensor_copy(dst, turned[:].rearrange("p u c -> p c u"))

        def second_layer(b, experts, n):
            piece = [i for i, (b0, b1) in enumerate(W2_PIECES) if b0 <= b < b1][0]
            local = b - W2_PIECES[piece][0]
            y = bank(n, [P, len(experts) * C])
            for i, e in enumerate(experts):
                nc.tensor.matmul_mx(
                    out=y[:, i * C : (i + 1) * C],
                    lhsT=w2w[piece][:, e, local * P : (local + 1) * P].bitcast(FP8X4),
                    lhsT_scale=w2s[4 * e : P, b * P : (b + 1) * P],
                    rhs=h_words[e].bitcast(FP8X4),
                    rhs_scale=h_scales[e][:],
                    start=True,
                    stop=True,
                )
            return window[b][:, experts[0] * C : (experts[-1] + 1) * C], y[:]

        def pick(b, r, lo, hi):
            product = keep.tile([P, hi - lo], F32, name=f"product{b}_{r}_{lo}")
            nc.vector.tensor_tensor(
                product[:], window[b][:].indirect(pos_sb[r][:, lo // 16 : hi // 16]), gate_sb[r][:, lo:hi], ALU.mult
            )
            return product

        def fetch(b, r, lo, hi):
            fetched = keep.tile([P, hi - lo], F32, name=f"fetched{b}_{r}_{lo}", tag=f"fetched{b}_{r}")
            nc.scalar.activation(fetched[:], window[b][:].indirect(pos_sb[r][:, lo // 16 : hi // 16]), ACT.Copy)
            return fetched

        def turn(fetched, n):
            chunks = fetched.shape[1] // P
            by_token = bank(n, [P, chunks, P])
            for c in range(chunks):
                nc.tensor.transpose(by_token[:, c, :], fetched[:, c * P : (c + 1) * P], ident[:])
            return by_token

        def weigh(b, r, lo, by_token, tag=None, product=None):
            chunks = by_token.shape[1]
            if product is None:
                product = keep.tile([P, chunks, P], F32, name=f"weighed{b}_{r}_{lo}", tag=tag or f"weighed{b}_{r}")
            for c in range(chunks):
                column = r * T // P + lo // P + c
                nc.scalar.activation(
                    product[:, c, :], by_token[:, c, :], ACT.Copy, scale=gate_t[:, column : column + 1]
                )
            return product

        def turn_back(first, second, n):
            chunks = first.shape[1]
            by_row = bank(n, [P, chunks, P])
            for r, product in enumerate((first, second)):
                for c in range(chunks):
                    nc.tensor.matmul(
                        by_row[:, c, :], product[:, c, :], ident[:],
                        start=(r == 0 and c == 0), stop=(r == 1 and c == chunks - 1), is_transpose=True,
                    )
            return by_row

        def store_sum(b, lo, by_row, tag, queue):
            width = by_row.shape[1] * P
            result = keep.tile([P, width], F32, name=f"result{b}_{lo}", tag=tag)
            nc.scalar.copy(result[:], by_row[:].rearrange("p c t -> p (c t)"))
            queue.dma_start(out=out[b * P : (b + 1) * P, lo : lo + width], in_=result[:])

        def add_into(result, b, first, second, lo, hi):
            nc.vector.tensor_tensor(result, first, second, ALU.add)
            nc.sync.dma_start(out=out[b * P : (b + 1) * P, lo:hi], in_=result)

        def add_on_vector(b, first, second, lo, hi, tag):
            result = keep.tile([P, hi - lo], F32, name=f"result{b}_{lo}", tag=tag)
            add_into(result[:], b, first, second, lo, hi)

        for e in range(E):
            gather_slots(e)

        sums0 = first_layer(0, 0)
        relu0 = relu_tile(0)
        nc.scalar.activation(relu0[:], by_byte(sums0), ACT.Relu)
        sums1 = first_layer(1, 1)
        turn_and_square(0, relu0, 5)
        sums2 = first_layer(2, 2)
        pairs1 = square_into_pairs(sums1)
        relu2 = relu_tile(2)
        nc.vector.tensor_scalar_max(relu2[:], by_byte(sums2), 0.0)
        sums3a = bank(3, [P, HALF_H])
        sums3b = bank(4, [P, HALF_H])
        for s in range(2):
            first_pass(LAST_EXPERT, s, w1w_last[s][:], sums3a, 0, HALF_H)
            first_pass(LAST_EXPERT, s, w1w_last[s][:], sums3b, HALF_H, H)
        relu3 = relu_tile(LAST_EXPERT)
        nc.scalar.activation(relu3[:, :, 0 : P // 2], by_byte(sums3a), ACT.Relu)
        nc.vector.tensor_scalar_max(relu3[:, :, P // 2 : P], by_byte(sums3b), 0.0)
        turn_and_square(2, relu2, 7)
        turn_pairs(1, pairs1, 2)
        turn_and_square(LAST_EXPERT, relu3, 5)

        h_early = keep.tile([P, LAST_EXPERT * C], U32, name="h_early", tag="w1w_last1", align_bytes=64)
        h_late = keep.tile([P, C], U32, name="h_late", align_bytes=64)
        for e in range(E):
            h_words[e] = h_early[:, e * C : (e + 1) * C] if e < LAST_EXPERT else h_late[:]
            nc.vector.quantize_mx(
                out=h_words[e].bitcast(FP8X4),
                scales=h_scales[e][:],
                in_=h_bf[e][:].rearrange("p c d -> p (c d)"),
            )

        nc.scalar.copy(*second_layer(0, list(range(LAST_EXPERT)), 0))
        nc.scalar.copy(*second_layer(1, list(range(LAST_EXPERT)), 2))
        nc.vector.tensor_copy(*second_layer(0, [LAST_EXPERT], 1))
        nc.scalar.copy(*second_layer(1, [LAST_EXPERT], 4))
        gate_turned = bank(4, [P, P])
        nc.tensor.transpose(gate_turned[:], gate_rows[:], ident[:])
        nc.scalar.copy(gate_t[:], gate_turned[:, 0 : 2 * T // P])

        def fill_window(b, n):
            nc.scalar.copy(*second_layer(b, list(range(E)), n))

        def on_vector(b, lo, hi, waiting, tag):
            first = pick(b, 0, lo, hi)
            if waiting:
                add_on_vector(*waiting)
            return (b, first[:], pick(b, 1, lo, hi)[:], lo, hi, tag)

        half = T // 2
        small, whole = pick(0, 0, 0, P), pick(1, 0, 0, T)
        waiting = (0, small[:], pick(0, 1, 0, P)[:], 0, P, "sum0")
        fill_window(2, 3)
        fill_window(3, 0)
        fill_window(4, 1)
        fetched0 = [fetch(0, r, P, T) for r in range(2)]
        turned0 = [turn(fetched0[0], 3), turn(fetched0[1], 0)]
        fetched3 = [fetch(3, r, 0, T) for r in range(2)]
        turned3 = turn(fetched3[0], 5)
        both = keep.tile([P, 6, P], F32, name="weighed0", tag="fetched3_0")
        first = weigh(0, 0, P, turned0[0], product=both[:, 0:3, :])
        second = weigh(0, 1, P, turned0[1], product=both[:, 3:6, :])
        first3 = weigh(3, 0, 0, turned3)
        other = pick(1, 1, 0, T)
        add_on_vector(*waiting)
        waiting = (1, whole[:], other[:], 0, T, "fetched0_0")
        waiting = on_vector(2, 0, T, waiting, "fetched0_1")
        fill_window(5, 2)
        fill_window(6, 4)
        sum0 = turn_back(first, second, 2)
        fill_window(7, 6)
        by_token = turn(fetched3[1], 4)
        store_sum(0, P, sum0, "result0", nc.sync)
        second = weigh(3, 1, 0, by_token)
        sum3 = turn_back(second, first3, 5)
        waiting = on_vector(4, 0, T, waiting, "fetched3_0")
        first = fetch(6, 0, 0, T)
        second = fetch(6, 1, 0, T)
        by_token = turn(first, 1)
        store_sum(3, 0, sum3, "fetched6_0", nc.sync)
        late = [turn(second[:, lo : lo + half], n) for lo, n in ((0, 3), (half, 2))]
        halves = []
        for i, lo in enumerate((0, half)):
            first = weigh(6, 0, lo, by_token[:, 2 * i : 2 * i + 2, :], f"weighed6_0_{i}")
            halves.append((first, weigh(6, 1, lo, late[i], f"weighed6_1_{i}")))
        waiting = on_vector(5, 0, T, waiting, "fetched3_1")
        whole = pick(7, 0, 0, T)
        add_on_vector(*waiting)
        ends = [pick(7, 1, lo, lo + half) for lo in (0, half)]
        result7 = keep.tile([P, T], F32, name="result7", tag="fetched6_1")
        for i, lo in enumerate((0, half)):
            by_row = turn_back(*halves[i], (0, 7)[i])
            store_sum(6, lo, by_row, f"end{i}", nc.scalar)
            add_into(result7[:, lo : lo + half], 7, whole[:, lo : lo + half], ends[i][:], lo, lo + half)
